import numpy as np
import ml_dtypes


def mxq(x, axis, fmt="e4m3"):
    dtype, down = {"e4m3": (ml_dtypes.float8_e4m3fn, 7), "e5m2": (ml_dtypes.float8_e5m2, 14)}[fmt]
    v = np.moveaxis(np.asarray(x, np.float32).astype(ml_dtypes.bfloat16).astype(np.float64), axis, -1)
    blocks = v.reshape(v.shape[:-1] + (-1, 32))
    amax = np.abs(blocks).max(-1, keepdims=True)
    byte = np.maximum(np.where(amax > 0, np.frexp(amax)[1] - 1 + 127, 0) - down, 1)
    scale = np.exp2(byte - 127.0)
    codes = (blocks / scale).astype(np.float32).astype(dtype).astype(np.float64)
    return np.moveaxis((codes * scale).reshape(v.shape), -1, axis)


WIDE = False


def mx_kscale(k):
    if not WIDE:
        return np.ones(k)
    levels = np.array([10, -10, 5, -5, 0])
    if k % 512:
        return np.exp2(np.random.permutation(np.resize(levels, k // 32))).repeat(32)
    a = np.empty((k // 512, 16))
    for p in range(k // 512):
        a[p, :8] = np.random.permutation(np.resize(levels, 8))
        for g in range(8):
            far = levels[np.abs(levels - a[p, g]) >= 10]
            a[p, g + 8] = far[np.random.randint(len(far))]
    return np.exp2(a.ravel()).repeat(32)


def f64(x):
    return np.asarray(x).astype(np.float64)


def striped(idx):
    return np.tile(idx.reshape(-1, 16).T, (8, 1)).astype(np.uint16)


def unstriped(offs):
    return offs[:16].T.reshape(-1).astype(np.int64)


E2M1 = np.array([0.0, 0.5, 1.0, 1.5, 2.0, 3.0, 4.0, 6.0, -0.0, -0.5, -1.0, -1.5, -2.0, -3.0, -4.0, -6.0])


def pack_weight(w, fmt):
    k, n = w.shape
    w = f64(np.asarray(w, np.float32).astype(ml_dtypes.bfloat16)).reshape(k // 32, 32, n)
    amax = np.abs(w).max(1)
    if fmt == "e4m3":
        byte = np.frexp(amax)[1] - 1 + 127 - 7
    else:
        mant, ex = np.frexp(amax / 6.0)
        byte = np.where(mant > 0.5, ex, ex - 1) + 127
    byte = np.clip(np.where(amax > 0, byte, 1), 1, 254)
    scaled = (w * np.exp2(127.0 - byte)[:, None, :]).reshape(k, n).astype(np.float32)
    by_word = np.ascontiguousarray(scaled.reshape(k // 512, 128, 4, n).transpose(0, 1, 3, 2))
    if fmt == "e4m3":
        words = by_word.astype(ml_dtypes.float8_e4m3fn).view(np.uint8)
    else:
        c = by_word.astype(ml_dtypes.float4_e2m1fn).view(np.uint8) & 0xF
        words = (c[..., 0::2] | (c[..., 1::2] << 4)).reshape(k // 512, 128, 2 * n)
    return np.ascontiguousarray(words), np.ascontiguousarray(byte.astype(np.uint8).reshape(k // 512, 16, n))


def unpack_weight(words, scales, fmt):
    g, _, n = scales.shape
    words = np.ascontiguousarray(words).reshape(g, 128, n, -1)
    if fmt == "e4m3":
        vals = words.view(ml_dtypes.float8_e4m3fn).astype(np.float64)
    else:
        nib = np.empty((g, 128, n, 4), np.uint8)
        nib[..., 0::2] = words & 0xF
        nib[..., 1::2] = words >> 4
        vals = E2M1[nib]
    vals = vals * np.repeat(np.exp2(scales.astype(np.float64) - 127.0), 8, axis=1)[..., None]
    return vals.transpose(0, 1, 3, 2).reshape(g * 512, n)


K, T, E, C, N = 1024, 1024, 8, 256, 128
M = 1024


def by_expert(wq, xq):
    return np.concatenate([wq[e].T @ xq[:, e * C:(e + 1) * C] for e in range(E)], axis=1)


def setup_inputs():
    n = np.random.standard_normal
    s = mx_kscale(K)[:, None]
    first = np.random.permutation(np.repeat(np.arange(E), T // E))
    second = (first + 1 + np.random.permutation(np.repeat(np.arange(E - 1), -(-T // (E - 1)))[:T])) % E
    while np.bincount(second, minlength=E).max() != T // E:
        load = np.bincount(second, minlength=E); hi, lo = int(load.argmax()), int(load.argmin())
        t = np.flatnonzero((second == hi) & (first != lo))[0]; second[t] = lo
    slot_token = np.empty(E * C, np.int64); pos = np.empty((2, T), np.int64); fill = np.zeros(E, np.int64)
    place = np.stack([np.random.permutation(C) for _ in range(E)])
    for r, deal in enumerate((first, second)):
        for t in np.random.permutation(T):
            e = deal[t]; j = e * C + place[e, fill[e]]; fill[e] += 1; slot_token[j] = t; pos[r, t] = j
    g = np.random.uniform(0.2, 0.8, T)
    w = [pack_weight(m, "e2m1") for m in n((E, K, N)) / np.sqrt(K) / s[None]]
    r = mx_kscale(M)[:, None]
    return {
        "uT": (n((M, T)) * r).astype(np.float32),
        "wu": (n((M, K)) / np.sqrt(M) / r * s.T).astype(np.float32),
        "w_words": np.stack([m[0] for m in w]),
        "w_scales": np.stack([m[1] for m in w]),
        "b": (0.3 * n((N, E))).astype(np.float32),
        "gate": np.stack([np.tile(g, (N, 1)), np.tile(1.0 - g, (N, 1))]).astype(np.float32),
        "offs": striped(slot_token),
        "pos1": striped(pos[0]),
        "pos2": striped(pos[1]),
    }


def reference(uT, wu, w_words, w_scales, b, gate, offs, pos1, pos2):
    idx = unstriped(offs)
    w = np.stack([unpack_weight(w_words[e], w_scales[e], "e2m1") for e in range(E)])
    x = mxq(f64(wu), 0, "e4m3").T @ mxq(f64(uT), 0, "e4m3")
    xq = mxq(x[:, idx], 0, "e4m3")
    y = by_expert(w, xq)
    y = y + np.repeat(f64(b), C, axis=1)
    return f64(gate[0]) * y[:, unstriped(pos1)] + f64(gate[1]) * y[:, unstriped(pos2)]

@@ -1,0 +1,271 @@
+from contextlib import ExitStack
+
+import concourse.mybir as mybir
+
+K, T, E, C, N, M = 1024, 1024, 8, 256, 128, 1024
+S = E * C
+
+FLOPS = 2 * M * K * T + 2 * K * N * S
+
+F32 = mybir.dt.float32
+BF16 = mybir.dt.bfloat16
+I32 = mybir.dt.int32
+U32 = mybir.dt.uint32
+U16 = mybir.dt.uint16
+U8 = mybir.dt.uint8
+FP8X4 = mybir.dt.float8_e4m3fn_x4
+FP4X4 = mybir.dt.float4_e2m1fn_x4
+MULT = mybir.AluOpType.mult
+ADD = mybir.AluOpType.add
+IDENTITY = mybir.ActivationFunctionType.Identity
+
+P = 128
+PACK = 4
+PASS = P * PACK
+PASSES = 2
+LIST_ROWS = 16
+
+
+def spans(widths):
+    out, start = [], 0
+    for w in widths:
+        out.append((start, start + w))
+        start += w
+    return out
+
+
+TOKEN_LOADS = spans([256, 256, 256, 128, 128])
+TOKEN_GROUPS = spans([256, 256, 256, 256])
+SLOT_CHUNKS = (spans([512, 512, 512, 512]), spans([512, 512, 512, 256, 256]))
+OUT_CHUNKS = spans([384, 384, 256])
+
+
+def tile_moe_prv_lin_bias_kernel(
+    tc, uT, wu, w_words, w_scales, b, gate, offs, pos1, pos2, out
+):
+    nc = tc.nc
+    with ExitStack() as ctx:
+        keep = ctx.enter_context(tc.tile_pool(name="keep", bufs=1))
+        stage = ctx.enter_context(tc.tile_pool(name="stage", bufs=4))
+        psum = ctx.enter_context(tc.psum_pool(name="psum", bufs=4))
+
+        offs_sb = keep.tile([P, S // LIST_ROWS], U16, name="offs_sb")
+        pos1_sb = keep.tile([P, T // LIST_ROWS], U16, name="pos1_sb")
+        pos2_sb = keep.tile([P, T // LIST_ROWS], U16, name="pos2_sb")
+        bias = keep.tile([P, E], F32, name="bias")
+        gates = keep.tile([P, 2, T], F32, name="gates")
+        w_codes = keep.tile([P, E * PASSES, 2 * N], U8, name="w_codes", align_bytes=64)
+        w_plane = keep.tile([P, E * PASSES, N], U8, name="w_plane", align_bytes=64)
+        wu_raw = [[keep.tile([P, PACK, PASS], F32, name=f"wu_raw{a}{f}", align_bytes=64) for f in range(PASSES)] for a in range(PASSES)]
+        u_raw = [[keep.tile([P, PACK, t1 - t0], F32, name=f"u_raw{i}{f}") for f in range(PASSES)]
+                 for i, (t0, t1) in enumerate(TOKEN_LOADS)]
+        wu_codes = keep.tile([P, PASSES, PASSES, PASS], U32, name="wu_codes", align_bytes=64)
+        wu_plane = keep.tile([P, PASSES, PASSES, PASS], U8, name="wu_plane", align_bytes=64)
+        u_codes = [keep.tile([P, T], U32, name=f"u_codes{f}", align_bytes=64) for f in range(PASSES)]
+        u_plane = keep.tile([P, PASSES, T], U8, name="u_plane", align_bytes=64)
+        x_pairs = [[keep.tile([P, T], U32, name=f"x_pairs{a}{h}", align_bytes=64) for h in range(2)] for a in range(PASSES)]
+        picked = {}
+        s_codes = keep.tile([P, PASSES, S], U32, name="s_codes", align_bytes=64)
+        s_plane = keep.tile([P, PASSES, S], U8, name="s_plane", align_bytes=64)
+        y = keep.tile([P, S], F32, name="y")
+        first = keep.tile([P, T], F32, name="first")
+        second = keep.tile([P, T], F32, name="second")
+        total = keep.tile([P, T], F32, name="total")
+
+        nc.vector.memset(w_plane[:].rearrange("p g n -> p (g n)").bitcast(I32), 0)
+
+        def load_wu(a):
+            for f in range(PASSES):
+                rows = wu[f * PASS:(f + 1) * PASS, a * PASS:(a + 1) * PASS]
+                nc.sync.dma_start(out=wu_raw[a][f][:], in_=rows.rearrange("(p j) c -> p j c", j=PACK))
+
+        load_wu(0)
+        nc.sync.dma_start(offs_sb[:], offs)
+        for i, (t0, t1) in enumerate(TOKEN_LOADS):
+            for f in range(PASSES):
+                rows = uT[f * PASS:(f + 1) * PASS, t0:t1]
+                nc.sync.dma_start(out=u_raw[i][f][:], in_=rows.rearrange("(p j) t -> p j t", j=PACK))
+        load_wu(1)
+        nc.sync.dma_start(
+            out=w_codes[:].bitcast(I32), in_=w_words.rearrange("e a p b -> p (e a) b").bitcast(I32)
+        )
+        scale_rows = w_scales.rearrange("e a q n -> q (e a) n").bitcast(I32)
+        for quad in range(4):
+            nc.sync.dma_start(
+                out=w_plane[32 * quad:32 * quad + 4, :, :].bitcast(I32), in_=scale_rows[4 * quad:4 * quad + 4]
+            )
+        nc.sync.dma_start(out=bias[:], in_=b)
+        nc.sync.dma_start(pos1_sb[:], pos1)
+        nc.sync.dma_start(pos2_sb[:], pos2)
+        nc.sync.dma_start(out=gates[:], in_=gate.rearrange("g p t -> p g t"))
+
+        def cast(on_vector, dst, src):
+            if on_vector:
+                nc.vector.tensor_copy(out=dst, in_=src)
+            else:
+                nc.scalar.copy(out=dst, in_=src)
+
+        def round_wu(a, f, on_vector):
+            grouped = keep.tile([P, PACK * PASS], BF16, name=f"shared{2 * a + f}", align_bytes=64)
+            cast(
+                on_vector,
+                grouped[:].rearrange("p (d m j) -> p m j d", d=PACK, j=PACK),
+                wu_raw[a][f][:].rearrange("p j (m d) -> p m j d", d=PACK),
+            )
+            return grouped
+
+        def quantize_wu(a, f, grouped):
+            nc.vector.quantize_mx(out=wu_codes[:, a, f, :].bitcast(FP8X4), scales=wu_plane[:, a, f, :], in_=grouped[:])
+
+        def round_u(i, f, on_vector):
+            t0, t1 = TOKEN_LOADS[i]
+            grouped = stage.tile([P, PACK * (t1 - t0)], BF16, name="narrow", align_bytes=64)
+            cast(
+                on_vector,
+                grouped[:].rearrange("p (c i j) -> p c j i", i=4, j=PACK),
+                u_raw[i][f][:].rearrange("p j (c i) -> p c j i", i=4),
+            )
+            return grouped
+
+        def quantize_u(i, f, grouped):
+            t0, t1 = TOKEN_LOADS[i]
+            nc.vector.quantize_mx(out=u_codes[f][:, t0:t1].bitcast(FP8X4), scales=u_plane[:, f, t0:t1], in_=grouped[:])
+
+        def project(a, h, t0, t1):
+            bank = psum.tile([P, 2, t1 - t0], F32, name="x_bank")
+            for e in range(2):
+                cols = slice((2 * h + e) * P, (2 * h + e + 1) * P)
+                for f in range(PASSES):
+                    nc.tensor.matmul_mx(
+                        out=bank[:, e, :],
+                        lhsT=wu_codes[:, a, f, cols].bitcast(FP8X4),
+                        lhsT_scale=wu_plane[:, a, f, cols],
+                        rhs=u_codes[f][:, t0:t1].bitcast(FP8X4),
+                        rhs_scale=u_plane[:, f, t0:t1],
+                        start=(f == 0),
+                        stop=(f == PASSES - 1),
+                    )
+            nc.scalar.copy(
+                out=x_pairs[a][h][:, t0:t1].bitcast(BF16).rearrange("p (t e) -> p t e", e=2),
+                in_=bank[:].rearrange("p e t -> p t e"),
+            )
+
+        def gather(a, h, i):
+            s0, s1 = SLOT_CHUNKS[a][i]
+            if h == 0:
+                tag = {(0, 0): "shared0", (0, 1): "shared1", (0, 2): "shared3", (0, 3): "shared2"}.get((a, i), f"picked{i}")
+                picked[a, i] = keep.tile([P, 2, s1 - s0], U32, name=tag, align_bytes=64)
+            nc.vector.tensor_copy(
+                out=picked[a, i][:, h, :],
+                in_=x_pairs[a][h][:].indirect(offs_sb[:, s0 // LIST_ROWS:s1 // LIST_ROWS]),
+            )
+
+        def interleave(a, i):
+            s0, s1 = SLOT_CHUNKS[a][i]
+            if (a, i) == (0, 0):
+                grouped = keep.tile([P, PACK * (s1 - s0)], BF16, name="wu_raw11", align_bytes=64)
+            elif a == 0 and i >= 2:
+                grouped = keep.tile([P, PACK * (s1 - s0)], BF16, name=f"u_codes{i - 2}", align_bytes=64)
+            else:
+                grouped = stage.tile([P, PACK * (s1 - s0)], BF16, name="wide", align_bytes=64)
+            nc.scalar.copy(
+                out=grouped[:].bitcast(F32).rearrange("p (s h) -> p s h", h=2),
+                in_=picked[a, i][:].bitcast(F32).rearrange("p h s -> p s h"),
+            )
+            return grouped
+
+        def quantize_slots(a, i, grouped):
+            s0, s1 = SLOT_CHUNKS[a][i]
+            nc.vector.quantize_mx(out=s_codes[:, a, s0:s1].bitcast(FP8X4), scales=s_plane[:, a, s0:s1], in_=grouped[:])
+
+        def expert(e):
+            bank = psum.tile([P, C], F32, name="y_bank")
+            for c0 in range(0, C, P):
+                slots = slice(e * C + c0, e * C + c0 + P)
+                for a in range(PASSES):
+                    nc.tensor.matmul_mx(
+                        out=bank[:, c0:c0 + P],
+                        lhsT=w_codes[:, e * PASSES + a, :].bitcast(FP4X4),
+                        lhsT_scale=w_plane[:, e * PASSES + a, :],
+                        rhs=s_codes[:, a, slots].bitcast(FP8X4),
+                        rhs_scale=s_plane[:, a, slots],
+                        start=(a == 0),
+                        stop=(a == PASSES - 1),
+                    )
+            nc.scalar.activation(out=y[:, e * C:(e + 1) * C], in_=bank[:], func=IDENTITY, bias=bias[:, e:e + 1])
+
+        g0 = round_wu(0, 0, False)
+        g1 = round_wu(0, 1, True)
+        quantize_wu(0, 0, g0)
+        quantize_wu(0, 1, g1)
+        for i, (t0, t1) in enumerate(TOKEN_LOADS):
+            g0 = round_u(i, 0, False)
+            g1 = round_u(i, 1, True)
+            quantize_u(i, 0, g0)
+            quantize_u(i, 1, g1)
+            for h in range(2):
+                project(0, h, t0, t1)
+
+        late = [round_wu(1, f, False) for f in range(PASSES)]
+        gather(0, 0, 0)
+        gather(0, 1, 0)
+        gather(0, 0, 1)
+        quantize_wu(1, 0, late[0])
+        gather(0, 1, 1)
+        quantize_wu(1, 1, late[1])
+        gather(0, 0, 2)
+        for h in range(2):
+            for t0, t1 in TOKEN_GROUPS:
+                project(1, h, t0, t1)
+        gather(0, 1, 2)
+        gather(0, 0, 3)
+        gather(0, 1, 3)
+        last = len(SLOT_CHUNKS[1]) - 1
+        for i in range(last + 1):
+            gather(1, 0, i)
+        for i in range(3):
+            quantize_slots(0, i, interleave(0, i))
+        gather(1, 1, 0)
+        ga = interleave(1, 0)
+        gather(1, 1, 1)
+        gb = interleave(1, 1)
+        quantize_slots(1, 0, ga)
+        expert(0)
+        expert(1)
+        gather(1, 1, 2)
+        gc = interleave(0, 3)
+        ga = interleave(1, 2)
+        quantize_slots(1, 1, gb)
+        expert(2)
+        expert(3)
+        gather(1, 1, 3)
+        gb = interleave(1, 3)
+        gather(1, 1, 4)
+        quantize_slots(0, 3, gc)
+        gc = interleave(1, 4)
+        quantize_slots(1, 2, ga)
+        expert(4)
+        expert(5)
+        quantize_slots(1, 3, gb)
+        expert(6)
+        quantize_slots(1, 4, gc)
+        expert(7)
+
+        def weigh(dst, pos_sb, g, t0, t1):
+            nc.vector.tensor_tensor(
+                out=dst[:, t0:t1],
+                in0=y[:].indirect(pos_sb[:, t0 // LIST_ROWS:t1 // LIST_ROWS]),
+                in1=gates[:, g, t0:t1],
+                op=MULT,
+            )
+
+        def finish(t0, t1):
+            nc.vector.tensor_tensor(out=total[:, t0:t1], in0=first[:, t0:t1], in1=second[:, t0:t1], op=ADD)
+            nc.sync.dma_start(out=out[:, t0:t1], in_=total[:, t0:t1])
+
+        for i, (t0, t1) in enumerate(OUT_CHUNKS):
+            weigh(first, pos1_sb, 0, t0, t1)
+            if i > 0:
+                finish(*OUT_CHUNKS[i - 1])
+            weigh(second, pos2_sb, 1, t0, t1)
+        finish(*OUT_CHUNKS[-1])

@@ -37,7 +37,7 @@ def spans(widths):
 TOKEN_LOADS = spans([256, 256, 256, 128, 128])
 TOKEN_GROUPS = spans([256, 256, 256, 256])
 SLOT_CHUNKS = (spans([512, 512, 512, 512]), spans([512, 512, 512, 256, 256]))
-OUT_CHUNKS = spans([384, 384, 256])
+OUT_CHUNKS = spans([512, 256, 256])
 
 
 def tile_moe_prv_lin_bias_kernel(
@@ -153,7 +153,7 @@ def tile_moe_prv_lin_bias_kernel(
         def gather(a, h, i):
             s0, s1 = SLOT_CHUNKS[a][i]
             if h == 0:
-                tag = {(0, 0): "shared0", (0, 1): "shared1", (0, 2): "shared3", (0, 3): "shared2"}.get((a, i), f"picked{i}")
+                tag = {(0, 0): "shared0", (0, 1): "shared1", (0, 2): "shared3", (0, 3): "shared2"}.get((a, i), f"ring{i % 2}" if i in (2, 3) else f"picked{i}")
                 picked[a, i] = keep.tile([P, 2, s1 - s0], U32, name=tag, align_bytes=64)
             nc.vector.tensor_copy(
                 out=picked[a, i][:, h, :],
@@ -166,6 +166,8 @@ def tile_moe_prv_lin_bias_kernel(
                 grouped = keep.tile([P, PACK * (s1 - s0)], BF16, name="wu_raw11", align_bytes=64)
             elif a == 0 and i >= 2:
                 grouped = keep.tile([P, PACK * (s1 - s0)], BF16, name=f"u_codes{i - 2}", align_bytes=64)
+            elif a == 1 and i <= 1:
+                grouped = keep.tile([P, PACK * (s1 - s0)], BF16, name=f"ring{i}", align_bytes=64)
             else:
                 grouped = stage.tile([P, PACK * (s1 - s0)], BF16, name="wide", align_bytes=64)
             nc.scalar.copy(
@@ -194,17 +196,31 @@ def tile_moe_prv_lin_bias_kernel(
                     )
             nc.scalar.activation(out=y[:, e * C:(e + 1) * C], in_=bank[:], func=IDENTITY, bias=bias[:, e:e + 1])
 
+        def expert_pass(bank, e, c0, a):
+            slots = slice(e * C + c0, e * C + c0 + P)
+            nc.tensor.matmul_mx(
+                out=bank,
+                lhsT=w_codes[:, e * PASSES + a, :].bitcast(FP4X4),
+                lhsT_scale=w_plane[:, e * PASSES + a, :],
+                rhs=s_codes[:, a, slots].bitcast(FP8X4),
+                rhs_scale=s_plane[:, a, slots],
+                start=(a == 0),
+                stop=(a == PASSES - 1),
+            )
+
         g0 = round_wu(0, 0, False)
         g1 = round_wu(0, 1, True)
         quantize_wu(0, 0, g0)
         quantize_wu(0, 1, g1)
         for i, (t0, t1) in enumerate(TOKEN_LOADS):
-            g0 = round_u(i, 0, False)
+            g0 = round_u(i, 0, i >= 2)
             g1 = round_u(i, 1, True)
             quantize_u(i, 0, g0)
             quantize_u(i, 1, g1)
-            for h in range(2):
-                project(0, h, t0, t1)
+            project(0, 0, t0, t1)
+            if i < 3:
+                project(0, 1, t0, t1)
+        project(0, 1, TOKEN_LOADS[3][0], T)
 
         late = [round_wu(1, f, False) for f in range(PASSES)]
         gather(0, 0, 0)
@@ -213,43 +229,52 @@ def tile_moe_prv_lin_bias_kernel(
         quantize_wu(1, 0, late[0])
         gather(0, 1, 1)
         quantize_wu(1, 1, late[1])
-        gather(0, 0, 2)
         for h in range(2):
             for t0, t1 in TOKEN_GROUPS:
                 project(1, h, t0, t1)
+        gather(0, 0, 2)
         gather(0, 1, 2)
         gather(0, 0, 3)
         gather(0, 1, 3)
-        last = len(SLOT_CHUNKS[1]) - 1
-        for i in range(last + 1):
-            gather(1, 0, i)
-        for i in range(3):
-            quantize_slots(0, i, interleave(0, i))
+        early = [interleave(0, i) for i in range(4)]
+        gather(1, 0, 0)
+        quantize_slots(0, 0, early[0])
         gather(1, 1, 0)
         ga = interleave(1, 0)
+        gather(1, 0, 1)
+        quantize_slots(0, 1, early[1])
         gather(1, 1, 1)
         gb = interleave(1, 1)
         quantize_slots(1, 0, ga)
         expert(0)
         expert(1)
+        quantize_slots(0, 2, early[2])
+        gather(1, 0, 2)
         gather(1, 1, 2)
-        gc = interleave(0, 3)
         ga = interleave(1, 2)
         quantize_slots(1, 1, gb)
         expert(2)
         expert(3)
+        quantize_slots(0, 3, early[3])
+        gather(1, 0, 3)
         gather(1, 1, 3)
         gb = interleave(1, 3)
-        gather(1, 1, 4)
-        quantize_slots(0, 3, gc)
-        gc = interleave(1, 4)
         quantize_slots(1, 2, ga)
         expert(4)
         expert(5)
+        opened = [psum.tile([P, P], F32, name="x_bank") for c0 in range(0, C, P)]
+        for bank, c0 in zip(opened, range(0, C, P)):
+            expert_pass(bank[:], E - 1, c0, 0)
+        gather(1, 0, 4)
+        gather(1, 1, 4)
+        gc = interleave(1, 4)
         quantize_slots(1, 3, gb)
         expert(6)
         quantize_slots(1, 4, gc)
-        expert(7)
+        for bank, c0 in zip(opened, range(0, C, P)):
+            expert_pass(bank[:], E - 1, c0, 1)
+            s0 = (E - 1) * C + c0
+            nc.scalar.activation(out=y[:, s0:s0 + P], in_=bank[:], func=IDENTITY, bias=bias[:, E - 1:E])
 
         def weigh(dst, pos_sb, g, t0, t1):
             nc.vector.tensor_tensor(
@@ -265,7 +290,7 @@ def tile_moe_prv_lin_bias_kernel(
 
         for i, (t0, t1) in enumerate(OUT_CHUNKS):
             weigh(first, pos1_sb, 0, t0, t1)
+            weigh(second, pos2_sb, 1, t0, t1)
             if i > 0:
                 finish(*OUT_CHUNKS[i - 1])
-            weigh(second, pos2_sb, 1, t0, t1)
         finish(*OUT_CHUNKS[-1])

@@ -37,7 +37,7 @@ def spans(widths):
 TOKEN_LOADS = spans([256, 256, 256, 128, 128])
 TOKEN_GROUPS = spans([256, 256, 256, 256])
 SLOT_CHUNKS = (spans([512, 512, 512, 512]), spans([512, 512, 512, 256, 256]))
-OUT_CHUNKS = spans([512, 256, 256])
+OUT_CHUNKS = spans([512, 384, 128])
 
 
 def tile_moe_prv_lin_bias_kernel(
@@ -47,7 +47,7 @@ def tile_moe_prv_lin_bias_kernel(
     with ExitStack() as ctx:
         keep = ctx.enter_context(tc.tile_pool(name="keep", bufs=1))
         stage = ctx.enter_context(tc.tile_pool(name="stage", bufs=4))
-        psum = ctx.enter_context(tc.psum_pool(name="psum", bufs=4))
+        psum = ctx.enter_context(tc.psum_pool(name="psum", bufs=8))
 
         offs_sb = keep.tile([P, S // LIST_ROWS], U16, name="offs_sb")
         pos1_sb = keep.tile([P, T // LIST_ROWS], U16, name="pos1_sb")
@@ -131,29 +131,38 @@ def tile_moe_prv_lin_bias_kernel(
             t0, t1 = TOKEN_LOADS[i]
             nc.vector.quantize_mx(out=u_codes[f][:, t0:t1].bitcast(FP8X4), scales=u_plane[:, f, t0:t1], in_=grouped[:])
 
-        def project(a, h, t0, t1):
-            bank = psum.tile([P, 2, t1 - t0], F32, name="x_bank")
-            for e in range(2):
-                cols = slice((2 * h + e) * P, (2 * h + e + 1) * P)
-                for f in range(PASSES):
-                    nc.tensor.matmul_mx(
-                        out=bank[:, e, :],
-                        lhsT=wu_codes[:, a, f, cols].bitcast(FP8X4),
-                        lhsT_scale=wu_plane[:, a, f, cols],
-                        rhs=u_codes[f][:, t0:t1].bitcast(FP8X4),
-                        rhs_scale=u_plane[:, f, t0:t1],
-                        start=(f == 0),
-                        stop=(f == PASSES - 1),
-                    )
+        def project_pass(bank, a, h, e, f, t0, t1):
+            cols = slice((2 * h + e) * P, (2 * h + e + 1) * P)
+            nc.tensor.matmul_mx(
+                out=bank[:, e, :],
+                lhsT=wu_codes[:, a, f, cols].bitcast(FP8X4),
+                lhsT_scale=wu_plane[:, a, f, cols],
+                rhs=u_codes[f][:, t0:t1].bitcast(FP8X4),
+                rhs_scale=u_plane[:, f, t0:t1],
+                start=(f == 0),
+                stop=(f == PASSES - 1),
+            )
+
+        def open_bank(a, h, t0, t1):
+            bank = psum.tile([P, 2, t1 - t0], F32, name="bank")
+            project_pass(bank, a, h, 0, 0, t0, t1)
+            return bank
+
+        def close_bank(bank, a, h, t0, t1):
+            for e, f in ((0, 1), (1, 0), (1, 1)):
+                project_pass(bank, a, h, e, f, t0, t1)
             nc.scalar.copy(
                 out=x_pairs[a][h][:, t0:t1].bitcast(BF16).rearrange("p (t e) -> p t e", e=2),
                 in_=bank[:].rearrange("p e t -> p t e"),
             )
 
+        def project(a, h, t0, t1):
+            close_bank(open_bank(a, h, t0, t1), a, h, t0, t1)
+
         def gather(a, h, i):
             s0, s1 = SLOT_CHUNKS[a][i]
             if h == 0:
-                tag = {(0, 0): "shared0", (0, 1): "shared1", (0, 2): "shared3", (0, 3): "shared2"}.get((a, i), f"ring{i % 2}" if i in (2, 3) else f"picked{i}")
+                tag = {(0, 0): "shared0", (0, 1): "shared1", (0, 2): "shared2", (0, 3): "shared3"}.get((a, i), f"ring{i % 2}" if i in (2, 3) else f"picked{i}")
                 picked[a, i] = keep.tile([P, 2, s1 - s0], U32, name=tag, align_bytes=64)
             nc.vector.tensor_copy(
                 out=picked[a, i][:, h, :],
@@ -162,26 +171,26 @@ def tile_moe_prv_lin_bias_kernel(
 
         def interleave(a, i):
             s0, s1 = SLOT_CHUNKS[a][i]
-            if (a, i) == (0, 0):
-                grouped = keep.tile([P, PACK * (s1 - s0)], BF16, name="wu_raw11", align_bytes=64)
-            elif a == 0 and i >= 2:
-                grouped = keep.tile([P, PACK * (s1 - s0)], BF16, name=f"u_codes{i - 2}", align_bytes=64)
-            elif a == 1 and i <= 1:
-                grouped = keep.tile([P, PACK * (s1 - s0)], BF16, name=f"ring{i}", align_bytes=64)
+            if a == 0 and i <= 1:
+                grouped = two_chunks[:, i, :]
+            elif a == 0:
+                grouped = keep.tile([P, PACK * (s1 - s0)], BF16, name=f"u_codes{i - 2}", align_bytes=64)[:]
+            elif i <= 1:
+                grouped = keep.tile([P, PACK * (s1 - s0)], BF16, name=f"ring{i}", align_bytes=64)[:]
             else:
-                grouped = stage.tile([P, PACK * (s1 - s0)], BF16, name="wide", align_bytes=64)
+                grouped = stage.tile([P, PACK * (s1 - s0)], BF16, name="wide", align_bytes=64)[:]
             nc.scalar.copy(
-                out=grouped[:].bitcast(F32).rearrange("p (s h) -> p s h", h=2),
+                out=grouped.bitcast(F32).rearrange("p (s h) -> p s h", h=2),
                 in_=picked[a, i][:].bitcast(F32).rearrange("p h s -> p s h"),
             )
             return grouped
 
         def quantize_slots(a, i, grouped):
             s0, s1 = SLOT_CHUNKS[a][i]
-            nc.vector.quantize_mx(out=s_codes[:, a, s0:s1].bitcast(FP8X4), scales=s_plane[:, a, s0:s1], in_=grouped[:])
+            nc.vector.quantize_mx(out=s_codes[:, a, s0:s1].bitcast(FP8X4), scales=s_plane[:, a, s0:s1], in_=grouped)
 
         def expert(e):
-            bank = psum.tile([P, C], F32, name="y_bank")
+            bank = psum.tile([P, C], F32, name="bank")
             for c0 in range(0, C, P):
                 slots = slice(e * C + c0, e * C + c0 + P)
                 for a in range(PASSES):
@@ -213,7 +222,7 @@ def tile_moe_prv_lin_bias_kernel(
         quantize_wu(0, 0, g0)
         quantize_wu(0, 1, g1)
         for i, (t0, t1) in enumerate(TOKEN_LOADS):
-            g0 = round_u(i, 0, i >= 2)
+            g0 = round_u(i, 0, i in (2, 4))
             g1 = round_u(i, 1, True)
             quantize_u(i, 0, g0)
             quantize_u(i, 1, g1)
@@ -226,43 +235,44 @@ def tile_moe_prv_lin_bias_kernel(
         gather(0, 0, 0)
         gather(0, 1, 0)
         gather(0, 0, 1)
-        quantize_wu(1, 0, late[0])
         gather(0, 1, 1)
-        quantize_wu(1, 1, late[1])
-        for h in range(2):
-            for t0, t1 in TOKEN_GROUPS:
-                project(1, h, t0, t1)
+        quantize_wu(1, 0, late[0])
+        banks = {(h, t0, t1): open_bank(1, h, t0, t1) for h in range(2) for t0, t1 in TOKEN_GROUPS}
         gather(0, 0, 2)
+        quantize_wu(1, 1, late[1])
+        two_chunks = keep.tile([P, 2, PACK * PASS], BF16, name="wu_raw11", align_bytes=64)
+        for (h, t0, t1), bank in banks.items():
+            close_bank(bank, 1, h, t0, t1)
         gather(0, 1, 2)
         gather(0, 0, 3)
         gather(0, 1, 3)
         early = [interleave(0, i) for i in range(4)]
-        gather(1, 0, 0)
         quantize_slots(0, 0, early[0])
+        quantize_slots(0, 1, early[1])
+        gather(1, 0, 0)
+        gather(1, 0, 1)
         gather(1, 1, 0)
         ga = interleave(1, 0)
-        gather(1, 0, 1)
-        quantize_slots(0, 1, early[1])
+        quantize_slots(0, 2, early[2])
         gather(1, 1, 1)
         gb = interleave(1, 1)
         quantize_slots(1, 0, ga)
         expert(0)
         expert(1)
-        quantize_slots(0, 2, early[2])
+        quantize_slots(0, 3, early[3])
         gather(1, 0, 2)
         gather(1, 1, 2)
         ga = interleave(1, 2)
         quantize_slots(1, 1, gb)
         expert(2)
         expert(3)
-        quantize_slots(0, 3, early[3])
         gather(1, 0, 3)
         gather(1, 1, 3)
         gb = interleave(1, 3)
         quantize_slots(1, 2, ga)
         expert(4)
         expert(5)
-        opened = [psum.tile([P, P], F32, name="x_bank") for c0 in range(0, C, P)]
+        opened = [psum.tile([P, P], F32, name="bank") for c0 in range(0, C, P)]
         for bank, c0 in zip(opened, range(0, C, P)):
             expert_pass(bank[:], E - 1, c0, 0)
         gather(1, 0, 4)

@@ -17,6 +17,7 @@ FP8X4 = mybir.dt.float8_e4m3fn_x4
 FP4X4 = mybir.dt.float4_e2m1fn_x4
 MULT = mybir.AluOpType.mult
 ADD = mybir.AluOpType.add
+COPY = mybir.ActivationFunctionType.Copy
 IDENTITY = mybir.ActivationFunctionType.Identity
 
 P = 128
@@ -36,6 +37,8 @@ def spans(widths):
 
 TOKEN_LOADS = spans([256, 256, 256, 128, 128])
 TOKEN_GROUPS = spans([256, 256, 256, 256])
+FIRST_GATHERS = spans([768, 512, 768])
+SECOND_GATHERS = spans([768, 768, 512])
 SLOT_CHUNKS = (spans([512, 512, 512, 512]), spans([512, 512, 512, 256, 256]))
 OUT_CHUNKS = spans([512, 384, 128])
 
@@ -63,8 +66,10 @@ def tile_moe_prv_lin_bias_kernel(
         wu_plane = keep.tile([P, PASSES, PASSES, PASS], U8, name="wu_plane", align_bytes=64)
         u_codes = [keep.tile([P, T], U32, name=f"u_codes{f}", align_bytes=64) for f in range(PASSES)]
         u_plane = keep.tile([P, PASSES, T], U8, name="u_plane", align_bytes=64)
-        x_pairs = [[keep.tile([P, T], U32, name=f"x_pairs{a}{h}", align_bytes=64) for h in range(2)] for a in range(PASSES)]
+        x_pairs = {(a, h): keep.tile([P, T], U32, name=f"x_pairs{a}{h}", align_bytes=64) for a, h in ((0, 0), (0, 1), (1, 0))}
+        x_planes = keep.tile([P, 2, T], BF16, name="x_planes", align_bytes=64)
         picked = {}
+        picked_second = keep.tile([P, 2, S], U32, name="picked_second", align_bytes=64)
         s_codes = keep.tile([P, PASSES, S], U32, name="s_codes", align_bytes=64)
         s_plane = keep.tile([P, PASSES, S], U8, name="s_plane", align_bytes=64)
         y = keep.tile([P, S], F32, name="y")
@@ -151,43 +156,58 @@ def tile_moe_prv_lin_bias_kernel(
         def close_bank(bank, a, h, t0, t1):
             for e, f in ((0, 1), (1, 0), (1, 1)):
                 project_pass(bank, a, h, e, f, t0, t1)
-            nc.scalar.copy(
-                out=x_pairs[a][h][:, t0:t1].bitcast(BF16).rearrange("p (t e) -> p t e", e=2),
-                in_=bank[:].rearrange("p e t -> p t e"),
-            )
+            if (a, h) in x_pairs:
+                nc.scalar.copy(
+                    out=x_pairs[a, h][:, t0:t1].bitcast(BF16).rearrange("p (t e) -> p t e", e=2),
+                    in_=bank[:].rearrange("p e t -> p t e"),
+                )
+            else:
+                nc.scalar.copy(out=x_planes[:, :, t0:t1], in_=bank[:])
 
         def project(a, h, t0, t1):
             close_bank(open_bank(a, h, t0, t1), a, h, t0, t1)
 
-        def gather(a, h, i):
-            s0, s1 = SLOT_CHUNKS[a][i]
+        def offsets(s0, s1):
+            return offs_sb[:, s0 // LIST_ROWS:s1 // LIST_ROWS]
+
+        def gather(dst, a, h, s0, s1):
+            nc.vector.tensor_copy(out=dst, in_=x_pairs[a, h][:].indirect(offsets(s0, s1)))
+
+        def gather_first(h, i):
+            s0, s1 = FIRST_GATHERS[i]
             if h == 0:
-                tag = {(0, 0): "shared0", (0, 1): "shared1", (0, 2): "shared2", (0, 3): "shared3"}.get((a, i), f"ring{i % 2}" if i in (2, 3) else f"picked{i}")
-                picked[a, i] = keep.tile([P, 2, s1 - s0], U32, name=tag, align_bytes=64)
-            nc.vector.tensor_copy(
-                out=picked[a, i][:, h, :],
-                in_=x_pairs[a][h][:].indirect(offs_sb[:, s0 // LIST_ROWS:s1 // LIST_ROWS]),
+                picked[i] = keep.tile([P, 2, s1 - s0], U32, name=("shared0", "shared2", "shared3")[i], align_bytes=64)
+            gather(picked[i][:, h, :], 0, h, s0, s1)
+
+        def gather_planes(c0):
+            halves = picked_second[:, 1, c0:c0 + C].bitcast(BF16).rearrange("p (s e) -> p e s", e=2)
+            for e in range(2):
+                nc.scalar.activation(out=halves[:, e, :], in_=x_planes[:, e, :].indirect(offsets(c0, c0 + C)), func=COPY)
+
+        def interleave(on_vector, grouped, pairs):
+            cast(
+                on_vector,
+                grouped.bitcast(F32).rearrange("p (s h) -> p s h", h=2),
+                pairs.bitcast(F32).rearrange("p h s -> p s h"),
             )
 
-        def interleave(a, i):
-            s0, s1 = SLOT_CHUNKS[a][i]
-            if a == 0 and i <= 1:
-                grouped = two_chunks[:, i, :]
-            elif a == 0:
-                grouped = keep.tile([P, PACK * (s1 - s0)], BF16, name=f"u_codes{i - 2}", align_bytes=64)[:]
-            elif i <= 1:
-                grouped = keep.tile([P, PACK * (s1 - s0)], BF16, name=f"ring{i}", align_bytes=64)[:]
-            else:
-                grouped = stage.tile([P, PACK * (s1 - s0)], BF16, name="wide", align_bytes=64)[:]
-            nc.scalar.copy(
-                out=grouped.bitcast(F32).rearrange("p (s h) -> p s h", h=2),
-                in_=picked[a, i][:].bitcast(F32).rearrange("p h s -> p s h"),
-            )
-            return grouped
+        def interleave_first(i):
+            s0, s1 = FIRST_GATHERS[i]
+            interleave(i > 0, first_grouped[:, PACK * s0:PACK * s1], picked[i][:])
+
+        def interleave_second(i):
+            s0, s1 = SLOT_CHUNKS[1][i]
+            grouped = stage.tile([P, PACK * (s1 - s0)], BF16, name="wide", align_bytes=64)
+            interleave(True, grouped[:], picked_second[:, :, s0:s1])
+            return grouped[:]
 
         def quantize_slots(a, i, grouped):
             s0, s1 = SLOT_CHUNKS[a][i]
             nc.vector.quantize_mx(out=s_codes[:, a, s0:s1].bitcast(FP8X4), scales=s_plane[:, a, s0:s1], in_=grouped)
+
+        def quantize_first(i):
+            s0, s1 = SLOT_CHUNKS[0][i]
+            quantize_slots(0, i, first_grouped[:, PACK * s0:PACK * s1])
 
         def expert(e):
             bank = psum.tile([P, C], F32, name="bank")
@@ -227,60 +247,55 @@ def tile_moe_prv_lin_bias_kernel(
             quantize_u(i, 0, g0)
             quantize_u(i, 1, g1)
             project(0, 0, t0, t1)
-            if i < 3:
+            if i < 2:
                 project(0, 1, t0, t1)
-        project(0, 1, TOKEN_LOADS[3][0], T)
+        for t0, t1 in TOKEN_GROUPS[2:]:
+            project(0, 1, t0, t1)
 
         late = [round_wu(1, f, False) for f in range(PASSES)]
-        gather(0, 0, 0)
-        gather(0, 1, 0)
-        gather(0, 0, 1)
-        gather(0, 1, 1)
+        gather_first(0, 0)
+        gather_first(1, 0)
         quantize_wu(1, 0, late[0])
         banks = {(h, t0, t1): open_bank(1, h, t0, t1) for h in range(2) for t0, t1 in TOKEN_GROUPS}
-        gather(0, 0, 2)
+        gather_first(0, 1)
+        gather_first(1, 1)
         quantize_wu(1, 1, late[1])
-        two_chunks = keep.tile([P, 2, PACK * PASS], BF16, name="wu_raw11", align_bytes=64)
+        first_grouped = keep.tile([P, PACK * S], BF16, name="wu_raw11", align_bytes=64)
         for (h, t0, t1), bank in banks.items():
             close_bank(bank, 1, h, t0, t1)
-        gather(0, 1, 2)
-        gather(0, 0, 3)
-        gather(0, 1, 3)
-        early = [interleave(0, i) for i in range(4)]
-        quantize_slots(0, 0, early[0])
-        quantize_slots(0, 1, early[1])
-        gather(1, 0, 0)
-        gather(1, 0, 1)
-        gather(1, 1, 0)
-        ga = interleave(1, 0)
-        quantize_slots(0, 2, early[2])
-        gather(1, 1, 1)
-        gb = interleave(1, 1)
-        quantize_slots(1, 0, ga)
-        expert(0)
-        expert(1)
-        quantize_slots(0, 3, early[3])
-        gather(1, 0, 2)
-        gather(1, 1, 2)
-        ga = interleave(1, 2)
-        quantize_slots(1, 1, gb)
-        expert(2)
-        expert(3)
-        gather(1, 0, 3)
-        gather(1, 1, 3)
-        gb = interleave(1, 3)
-        quantize_slots(1, 2, ga)
-        expert(4)
-        expert(5)
+        gather_first(0, 2)
+        gather_first(1, 2)
+        interleave_first(0)
+        interleave_first(1)
+        quantize_first(0)
+        interleave_first(2)
+        quantize_first(1)
+        for s0, s1 in SECOND_GATHERS:
+            gather(picked_second[:, 0, s0:s1], 1, 0, s0, s1)
+        for c0 in range(0, S, C):
+            gather_planes(c0)
+        quantize_first(2)
+        ga = interleave_second(0)
+        quantize_first(3)
         opened = [psum.tile([P, P], F32, name="bank") for c0 in range(0, C, P)]
         for bank, c0 in zip(opened, range(0, C, P)):
             expert_pass(bank[:], E - 1, c0, 0)
-        gather(1, 0, 4)
-        gather(1, 1, 4)
-        gc = interleave(1, 4)
+        gb = interleave_second(1)
+        quantize_slots(1, 0, ga)
+        expert(0)
+        expert(1)
+        ga = interleave_second(2)
+        quantize_slots(1, 1, gb)
+        expert(2)
+        expert(3)
+        gb = interleave_second(3)
+        quantize_slots(1, 2, ga)
+        expert(4)
+        expert(5)
+        ga = interleave_second(4)
         quantize_slots(1, 3, gb)
         expert(6)
-        quantize_slots(1, 4, gc)
+        quantize_slots(1, 4, ga)
         for bank, c0 in zip(opened, range(0, C, P)):
             expert_pass(bank[:], E - 1, c0, 1)
             s0 = (E - 1) * C + c0

@@ -35,7 +35,8 @@ def spans(widths):
     return out
 
 
-TOKEN_LOADS = spans([256, 256, 256, 128, 128])
+TOKEN_LOADS = [(0, 0, 256), (1, 0, 256), (0, 256, 512), (1, 256, 512), (0, 512, 768), (1, 512, 768), (0, 768, 1024),
+               (1, 768, 896), (1, 896, 1024)]
 TOKEN_GROUPS = spans([256, 256, 256, 256])
 FIRST_GATHERS = spans([768, 512, 768])
 SECOND_GATHERS = spans([768, 768, 512])
@@ -60,8 +61,7 @@ def tile_moe_prv_lin_bias_kernel(
         w_codes = keep.tile([P, E * PASSES, 2 * N], U8, name="w_codes", align_bytes=64)
         w_plane = keep.tile([P, E * PASSES, N], U8, name="w_plane", align_bytes=64)
         wu_raw = [[keep.tile([P, PACK, PASS], F32, name=f"wu_raw{a}{f}", align_bytes=64) for f in range(PASSES)] for a in range(PASSES)]
-        u_raw = [[keep.tile([P, PACK, t1 - t0], F32, name=f"u_raw{i}{f}") for f in range(PASSES)]
-                 for i, (t0, t1) in enumerate(TOKEN_LOADS)]
+        u_raw = [keep.tile([P, PACK, t1 - t0], F32, name=f"u_raw{i}") for i, (f, t0, t1) in enumerate(TOKEN_LOADS)]
         wu_codes = keep.tile([P, PASSES, PASSES, PASS], U32, name="wu_codes", align_bytes=64)
         wu_plane = keep.tile([P, PASSES, PASSES, PASS], U8, name="wu_plane", align_bytes=64)
         u_codes = [keep.tile([P, T], U32, name=f"u_codes{f}", align_bytes=64) for f in range(PASSES)]
@@ -79,18 +79,23 @@ def tile_moe_prv_lin_bias_kernel(
 
         nc.vector.memset(w_plane[:].rearrange("p g n -> p (g n)").bitcast(I32), 0)
 
-        def load_wu(a):
-            for f in range(PASSES):
-                rows = wu[f * PASS:(f + 1) * PASS, a * PASS:(a + 1) * PASS]
-                nc.sync.dma_start(out=wu_raw[a][f][:], in_=rows.rearrange("(p j) c -> p j c", j=PACK))
+        def load_wu(a, f):
+            rows = wu[f * PASS:(f + 1) * PASS, a * PASS:(a + 1) * PASS]
+            nc.sync.dma_start(out=wu_raw[a][f][:], in_=rows.rearrange("(p j) c -> p j c", j=PACK))
 
-        load_wu(0)
+        def load_u(i):
+            f, t0, t1 = TOKEN_LOADS[i]
+            rows = uT[f * PASS:(f + 1) * PASS, t0:t1]
+            nc.sync.dma_start(out=u_raw[i][:], in_=rows.rearrange("(p j) t -> p j t", j=PACK))
+
+        load_u(0)
+        for f in range(PASSES):
+            load_wu(0, f)
+        for i in range(1, len(TOKEN_LOADS)):
+            load_u(i)
         nc.sync.dma_start(offs_sb[:], offs)
-        for i, (t0, t1) in enumerate(TOKEN_LOADS):
-            for f in range(PASSES):
-                rows = uT[f * PASS:(f + 1) * PASS, t0:t1]
-                nc.sync.dma_start(out=u_raw[i][f][:], in_=rows.rearrange("(p j) t -> p j t", j=PACK))
-        load_wu(1)
+        for f in range(PASSES):
+            load_wu(1, f)
         nc.sync.dma_start(
             out=w_codes[:].bitcast(I32), in_=w_words.rearrange("e a p b -> p (e a) b").bitcast(I32)
         )
@@ -112,28 +117,30 @@ def tile_moe_prv_lin_bias_kernel(
 
         def round_wu(a, f, on_vector):
             grouped = keep.tile([P, PACK * PASS], BF16, name=f"shared{2 * a + f}", align_bytes=64)
-            cast(
-                on_vector,
-                grouped[:].rearrange("p (d m j) -> p m j d", d=PACK, j=PACK),
-                wu_raw[a][f][:].rearrange("p j (m d) -> p m j d", d=PACK),
-            )
+            dst = grouped[:].rearrange("p (d m j) -> p m j d", d=PACK, j=PACK)
+            src = wu_raw[a][f][:].rearrange("p j (m d) -> p m j d", d=PACK)
+            if on_vector is None:
+                cast(False, dst[:, :, :, :2], src[:, :, :, :2])
+                cast(True, dst[:, :, :, 2:], src[:, :, :, 2:])
+            else:
+                cast(on_vector, dst, src)
             return grouped
 
         def quantize_wu(a, f, grouped):
             nc.vector.quantize_mx(out=wu_codes[:, a, f, :].bitcast(FP8X4), scales=wu_plane[:, a, f, :], in_=grouped[:])
 
-        def round_u(i, f, on_vector):
-            t0, t1 = TOKEN_LOADS[i]
+        def round_u(i, on_vector):
+            f, t0, t1 = TOKEN_LOADS[i]
             grouped = stage.tile([P, PACK * (t1 - t0)], BF16, name="narrow", align_bytes=64)
             cast(
                 on_vector,
                 grouped[:].rearrange("p (c i j) -> p c j i", i=4, j=PACK),
-                u_raw[i][f][:].rearrange("p j (c i) -> p c j i", i=4),
+                u_raw[i][:].rearrange("p j (c i) -> p c j i", i=4),
             )
             return grouped
 
-        def quantize_u(i, f, grouped):
-            t0, t1 = TOKEN_LOADS[i]
+        def quantize_u(i, grouped):
+            f, t0, t1 = TOKEN_LOADS[i]
             nc.vector.quantize_mx(out=u_codes[f][:, t0:t1].bitcast(FP8X4), scales=u_plane[:, f, t0:t1], in_=grouped[:])
 
         def project_pass(bank, a, h, e, f, t0, t1):
@@ -237,19 +244,22 @@ def tile_moe_prv_lin_bias_kernel(
                 stop=(a == PASSES - 1),
             )
 
-        g0 = round_wu(0, 0, False)
-        g1 = round_wu(0, 1, True)
-        quantize_wu(0, 0, g0)
-        quantize_wu(0, 1, g1)
-        for i, (t0, t1) in enumerate(TOKEN_LOADS):
-            g0 = round_u(i, 0, i in (2, 4))
-            g1 = round_u(i, 1, True)
-            quantize_u(i, 0, g0)
-            quantize_u(i, 1, g1)
-            project(0, 0, t0, t1)
-            if i < 2:
-                project(0, 1, t0, t1)
-        for t0, t1 in TOKEN_GROUPS[2:]:
+        quantize_u(0, round_u(0, True))
+        quantize_wu(0, 0, round_wu(0, 0, True))
+        weights = round_wu(0, 1, None)
+        tokens = round_u(1, True)
+        quantize_wu(0, 1, weights)
+        quantize_u(1, tokens)
+        for h in range(2):
+            project(0, h, *TOKEN_GROUPS[0])
+        for i in range(2, len(TOKEN_LOADS)):
+            f, t0, t1 = TOKEN_LOADS[i]
+            quantize_u(i, round_u(i, i != 2))
+            if f == 1:
+                project(0, 0, t0, t1)
+                if t1 <= 768:
+                    project(0, 1, t0, t1)
+        for t0, t1 in TOKEN_GROUPS[3:]:
             project(0, 1, t0, t1)
 
         late = [round_wu(1, f, False) for f in range(PASSES)]

@@ -25,6 +25,9 @@ PACK = 4
 PASS = P * PACK
 PASSES = 2
 LIST_ROWS = 16
+GROUP = 256
+QUADRANTS = 4
+RUN = 4
 
 
 def spans(widths):
@@ -35,9 +38,11 @@ def spans(widths):
     return out
 
 
-TOKEN_LOADS = [(0, 0, 256), (1, 0, 256), (0, 256, 512), (1, 256, 512), (0, 512, 768), (1, 512, 768), (0, 768, 1024),
-               (1, 768, 896), (1, 896, 1024)]
-TOKEN_GROUPS = spans([256, 256, 256, 256])
+TOKEN_GROUPS = spans([GROUP] * (T // GROUP))
+TOKEN_LOADS = [(f, t0, t1) for t0, t1 in TOKEN_GROUPS for f in range(PASSES)][:-1] + [
+    (1, T - GROUP, T - GROUP // 2),
+    (1, T - GROUP // 2, T),
+]
 FIRST_GATHERS = spans([768, 512, 768])
 SECOND_GATHERS = spans([768, 768, 512])
 SLOT_CHUNKS = (spans([512, 512, 512, 512]), spans([512, 512, 512, 256, 256]))
@@ -60,15 +65,18 @@ def tile_moe_prv_lin_bias_kernel(
         gates = keep.tile([P, 2, T], F32, name="gates")
         w_codes = keep.tile([P, E * PASSES, 2 * N], U8, name="w_codes", align_bytes=64)
         w_plane = keep.tile([P, E * PASSES, N], U8, name="w_plane", align_bytes=64)
-        wu_raw = [[keep.tile([P, PACK, PASS], F32, name=f"wu_raw{a}{f}", align_bytes=64) for f in range(PASSES)] for a in range(PASSES)]
+        wu_raw = [
+            [keep.tile([P, PACK, PASS], F32, name=f"wu_raw{a}{f}", align_bytes=64) for f in range(PASSES)]
+            for a in range(PASSES)
+        ]
         u_raw = [keep.tile([P, PACK, t1 - t0], F32, name=f"u_raw{i}") for i, (f, t0, t1) in enumerate(TOKEN_LOADS)]
         wu_codes = keep.tile([P, PASSES, PASSES, PASS], U32, name="wu_codes", align_bytes=64)
         wu_plane = keep.tile([P, PASSES, PASSES, PASS], U8, name="wu_plane", align_bytes=64)
-        u_codes = [keep.tile([P, T], U32, name=f"u_codes{f}", align_bytes=64) for f in range(PASSES)]
-        u_plane = keep.tile([P, PASSES, T], U8, name="u_plane", align_bytes=64)
+        u_codes = keep.tile([P, PASSES * T], U32, name="u_codes", align_bytes=64)
+        u_plane = keep.tile([P, PASSES * T], U8, name="u_plane", align_bytes=64)
         x_pairs = {(a, h): keep.tile([P, T], U32, name=f"x_pairs{a}{h}", align_bytes=64) for a, h in ((0, 0), (0, 1), (1, 0))}
-        x_planes = keep.tile([P, 2, T], BF16, name="x_planes", align_bytes=64)
-        picked = {}
+        x_rows = keep.tile([P, 2, T], BF16, name="x_rows", align_bytes=64)
+        picked_first = {}
         picked_second = keep.tile([P, 2, S], U32, name="picked_second", align_bytes=64)
         s_codes = keep.tile([P, PASSES, S], U32, name="s_codes", align_bytes=64)
         s_plane = keep.tile([P, PASSES, S], U8, name="s_plane", align_bytes=64)
@@ -100,7 +108,7 @@ def tile_moe_prv_lin_bias_kernel(
             out=w_codes[:].bitcast(I32), in_=w_words.rearrange("e a p b -> p (e a) b").bitcast(I32)
         )
         scale_rows = w_scales.rearrange("e a q n -> q (e a) n").bitcast(I32)
-        for quad in range(4):
+        for quad in range(QUADRANTS):
             nc.sync.dma_start(
                 out=w_plane[32 * quad:32 * quad + 4, :, :].bitcast(I32), in_=scale_rows[4 * quad:4 * quad + 4]
             )
@@ -109,39 +117,41 @@ def tile_moe_prv_lin_bias_kernel(
         nc.sync.dma_start(pos2_sb[:], pos2)
         nc.sync.dma_start(out=gates[:], in_=gate.rearrange("g p t -> p g t"))
 
-        def cast(on_vector, dst, src):
-            if on_vector:
-                nc.vector.tensor_copy(out=dst, in_=src)
-            else:
-                nc.scalar.copy(out=dst, in_=src)
+        on_vector = nc.vector.tensor_copy
+        on_scalar = nc.scalar.copy
 
-        def round_wu(a, f, on_vector):
-            grouped = keep.tile([P, PACK * PASS], BF16, name=f"shared{2 * a + f}", align_bytes=64)
+        def round_wu(a, f, shares):
+            grouped = keep.tile([P, PACK * PASS], BF16, name=f"shared{PASSES * a + f}", align_bytes=64)
             dst = grouped[:].rearrange("p (d m j) -> p m j d", d=PACK, j=PACK)
             src = wu_raw[a][f][:].rearrange("p j (m d) -> p m j d", d=PACK)
-            if on_vector is None:
-                cast(False, dst[:, :, :, :2], src[:, :, :, :2])
-                cast(True, dst[:, :, :, 2:], src[:, :, :, 2:])
-            else:
-                cast(on_vector, dst, src)
+            for copy, ds in shares:
+                copy(out=dst[:, :, :, ds], in_=src[:, :, :, ds])
             return grouped
 
         def quantize_wu(a, f, grouped):
             nc.vector.quantize_mx(out=wu_codes[:, a, f, :].bitcast(FP8X4), scales=wu_plane[:, a, f, :], in_=grouped[:])
 
-        def round_u(i, on_vector):
-            f, t0, t1 = TOKEN_LOADS[i]
-            grouped = stage.tile([P, PACK * (t1 - t0)], BF16, name="narrow", align_bytes=64)
-            cast(
-                on_vector,
-                grouped[:].rearrange("p (c i j) -> p c j i", i=4, j=PACK),
-                u_raw[i][:].rearrange("p j (c i) -> p c j i", i=4),
+        def u_columns(f, t0, width):
+            start = PASSES * GROUP * (t0 // GROUP) + f * GROUP + t0 % GROUP
+            return slice(start, start + width)
+
+        def round_u(i, copy, grouped):
+            copy(
+                out=grouped.rearrange("p (c i j) -> p c j i", i=RUN, j=PACK),
+                in_=u_raw[i][:].rearrange("p j (c i) -> p c j i", i=RUN),
             )
+
+        def round_loads(i, copies):
+            widths = [PACK * (t1 - t0) for f, t0, t1 in TOKEN_LOADS[i:i + len(copies)]]
+            grouped = stage.tile([P, sum(widths)], BF16, name="narrow", align_bytes=64)
+            for n, (copy, (x0, x1)) in enumerate(zip(copies, spans(widths))):
+                round_u(i + n, copy, grouped[:, x0:x1])
             return grouped
 
         def quantize_u(i, grouped):
             f, t0, t1 = TOKEN_LOADS[i]
-            nc.vector.quantize_mx(out=u_codes[f][:, t0:t1].bitcast(FP8X4), scales=u_plane[:, f, t0:t1], in_=grouped[:])
+            cols = u_columns(f, t0, grouped.shape[1] // PACK)
+            nc.vector.quantize_mx(out=u_codes[:, cols].bitcast(FP8X4), scales=u_plane[:, cols], in_=grouped[:])
 
         def project_pass(bank, a, h, e, f, t0, t1):
             cols = slice((2 * h + e) * P, (2 * h + e + 1) * P)
@@ -149,8 +159,8 @@ def tile_moe_prv_lin_bias_kernel(
                 out=bank[:, e, :],
                 lhsT=wu_codes[:, a, f, cols].bitcast(FP8X4),
                 lhsT_scale=wu_plane[:, a, f, cols],
-                rhs=u_codes[f][:, t0:t1].bitcast(FP8X4),
-                rhs_scale=u_plane[:, f, t0:t1],
+                rhs=u_codes[:, u_columns(f, t0, t1 - t0)].bitcast(FP8X4),
+                rhs_scale=u_plane[:, u_columns(f, t0, t1 - t0)],
                 start=(f == 0),
                 stop=(f == PASSES - 1),
             )
@@ -169,7 +179,7 @@ def tile_moe_prv_lin_bias_kernel(
                     in_=bank[:].rearrange("p e t -> p t e"),
                 )
             else:
-                nc.scalar.copy(out=x_planes[:, :, t0:t1], in_=bank[:])
+                nc.scalar.copy(out=x_rows[:, :, t0:t1], in_=bank[:])
 
         def project(a, h, t0, t1):
             close_bank(open_bank(a, h, t0, t1), a, h, t0, t1)
@@ -180,32 +190,31 @@ def tile_moe_prv_lin_bias_kernel(
         def gather(dst, a, h, s0, s1):
             nc.vector.tensor_copy(out=dst, in_=x_pairs[a, h][:].indirect(offsets(s0, s1)))
 
-        def gather_first(h, i):
+        def gather_first(i, buffer):
             s0, s1 = FIRST_GATHERS[i]
-            if h == 0:
-                picked[i] = keep.tile([P, 2, s1 - s0], U32, name=("shared0", "shared2", "shared3")[i], align_bytes=64)
-            gather(picked[i][:, h, :], 0, h, s0, s1)
+            picked_first[i] = keep.tile([P, 2, s1 - s0], U32, name=buffer, align_bytes=64)
+            for h in range(2):
+                gather(picked_first[i][:, h, :], 0, h, s0, s1)
 
-        def gather_planes(c0):
+        def gather_rows(c0):
             halves = picked_second[:, 1, c0:c0 + C].bitcast(BF16).rearrange("p (s e) -> p e s", e=2)
             for e in range(2):
-                nc.scalar.activation(out=halves[:, e, :], in_=x_planes[:, e, :].indirect(offsets(c0, c0 + C)), func=COPY)
+                nc.scalar.activation(out=halves[:, e, :], in_=x_rows[:, e, :].indirect(offsets(c0, c0 + C)), func=COPY)
 
-        def interleave(on_vector, grouped, pairs):
-            cast(
-                on_vector,
-                grouped.bitcast(F32).rearrange("p (s h) -> p s h", h=2),
-                pairs.bitcast(F32).rearrange("p h s -> p s h"),
+        def interleave(copy, grouped, pairs):
+            copy(
+                out=grouped.bitcast(F32).rearrange("p (s h) -> p s h", h=2),
+                in_=pairs.bitcast(F32).rearrange("p h s -> p s h"),
             )
 
-        def interleave_first(i):
+        def interleave_first(i, copy):
             s0, s1 = FIRST_GATHERS[i]
-            interleave(i > 0, first_grouped[:, PACK * s0:PACK * s1], picked[i][:])
+            interleave(copy, first_grouped[:, PACK * s0:PACK * s1], picked_first[i][:])
 
         def interleave_second(i):
             s0, s1 = SLOT_CHUNKS[1][i]
             grouped = stage.tile([P, PACK * (s1 - s0)], BF16, name="wide", align_bytes=64)
-            interleave(True, grouped[:], picked_second[:, :, s0:s1])
+            interleave(on_vector, grouped[:], picked_second[:, :, s0:s1])
             return grouped[:]
 
         def quantize_slots(a, i, grouped):
@@ -216,106 +225,93 @@ def tile_moe_prv_lin_bias_kernel(
             s0, s1 = SLOT_CHUNKS[0][i]
             quantize_slots(0, i, first_grouped[:, PACK * s0:PACK * s1])
 
-        def expert(e):
-            bank = psum.tile([P, C], F32, name="bank")
-            for c0 in range(0, C, P):
-                slots = slice(e * C + c0, e * C + c0 + P)
-                for a in range(PASSES):
-                    nc.tensor.matmul_mx(
-                        out=bank[:, c0:c0 + P],
-                        lhsT=w_codes[:, e * PASSES + a, :].bitcast(FP4X4),
-                        lhsT_scale=w_plane[:, e * PASSES + a, :],
-                        rhs=s_codes[:, a, slots].bitcast(FP8X4),
-                        rhs_scale=s_plane[:, a, slots],
-                        start=(a == 0),
-                        stop=(a == PASSES - 1),
-                    )
-            nc.scalar.activation(out=y[:, e * C:(e + 1) * C], in_=bank[:], func=IDENTITY, bias=bias[:, e:e + 1])
-
-        def expert_pass(bank, e, c0, a):
-            slots = slice(e * C + c0, e * C + c0 + P)
+        def expert_pass(sums, expert_index, c0, a):
+            slots = slice(expert_index * C + c0, expert_index * C + c0 + P)
             nc.tensor.matmul_mx(
-                out=bank,
-                lhsT=w_codes[:, e * PASSES + a, :].bitcast(FP4X4),
-                lhsT_scale=w_plane[:, e * PASSES + a, :],
+                out=sums,
+                lhsT=w_codes[:, expert_index * PASSES + a, :].bitcast(FP4X4),
+                lhsT_scale=w_plane[:, expert_index * PASSES + a, :],
                 rhs=s_codes[:, a, slots].bitcast(FP8X4),
                 rhs_scale=s_plane[:, a, slots],
                 start=(a == 0),
                 stop=(a == PASSES - 1),
             )
 
-        quantize_u(0, round_u(0, True))
-        quantize_wu(0, 0, round_wu(0, 0, True))
-        weights = round_wu(0, 1, None)
-        tokens = round_u(1, True)
+        def add_bias(sums, expert_index, c0, c1):
+            s0 = expert_index * C
+            nc.scalar.activation(
+                out=y[:, s0 + c0:s0 + c1], in_=sums, func=IDENTITY, bias=bias[:, expert_index:expert_index + 1]
+            )
+
+        def expert(expert_index):
+            bank = psum.tile([P, C], F32, name="bank")
+            for c0 in range(0, C, P):
+                for a in range(PASSES):
+                    expert_pass(bank[:, c0:c0 + P], expert_index, c0, a)
+            add_bias(bank[:], expert_index, 0, C)
+
+        halves = [(on_scalar, slice(0, 2)), (on_vector, slice(2, PACK))]
+        quantize_u(0, round_loads(0, [on_vector]))
+        quantize_wu(0, 0, round_wu(0, 0, halves))
+        weights = round_wu(0, 1, halves)
+        tokens = round_loads(1, [on_vector])
         quantize_wu(0, 1, weights)
         quantize_u(1, tokens)
         for h in range(2):
             project(0, h, *TOKEN_GROUPS[0])
-        for i in range(2, len(TOKEN_LOADS)):
+        for g, copies in ((1, [on_scalar, on_vector]), (2, [on_vector, on_vector])):
+            quantize_u(PASSES * g, round_loads(PASSES * g, copies))
+            for h in range(2):
+                project(0, h, *TOKEN_GROUPS[g])
+        for i in range(PASSES * (len(TOKEN_GROUPS) - 1), len(TOKEN_LOADS)):
             f, t0, t1 = TOKEN_LOADS[i]
-            quantize_u(i, round_u(i, i != 2))
-            if f == 1:
+            quantize_u(i, round_loads(i, [on_vector]))
+            if f == PASSES - 1:
                 project(0, 0, t0, t1)
-                if t1 <= 768:
-                    project(0, 1, t0, t1)
-        for t0, t1 in TOKEN_GROUPS[3:]:
-            project(0, 1, t0, t1)
+        project(0, 1, *TOKEN_GROUPS[-1])
 
-        late = [round_wu(1, f, False) for f in range(PASSES)]
-        gather_first(0, 0)
-        gather_first(1, 0)
+        late = [round_wu(1, f, [(on_scalar, slice(0, PACK))]) for f in range(PASSES)]
+        gather_first(0, "shared0")
         quantize_wu(1, 0, late[0])
         banks = {(h, t0, t1): open_bank(1, h, t0, t1) for h in range(2) for t0, t1 in TOKEN_GROUPS}
-        gather_first(0, 1)
-        gather_first(1, 1)
+        gather_first(1, "shared2")
         quantize_wu(1, 1, late[1])
         first_grouped = keep.tile([P, PACK * S], BF16, name="wu_raw11", align_bytes=64)
         for (h, t0, t1), bank in banks.items():
             close_bank(bank, 1, h, t0, t1)
-        gather_first(0, 2)
-        gather_first(1, 2)
-        interleave_first(0)
-        interleave_first(1)
+        gather_first(2, "shared3")
+        interleave_first(0, on_scalar)
+        interleave_first(1, on_vector)
         quantize_first(0)
-        interleave_first(2)
+        interleave_first(2, on_vector)
         quantize_first(1)
+
         for s0, s1 in SECOND_GATHERS:
             gather(picked_second[:, 0, s0:s1], 1, 0, s0, s1)
         for c0 in range(0, S, C):
-            gather_planes(c0)
+            gather_rows(c0)
         quantize_first(2)
-        ga = interleave_second(0)
+        grouped = interleave_second(0)
         quantize_first(3)
         opened = [psum.tile([P, P], F32, name="bank") for c0 in range(0, C, P)]
         for bank, c0 in zip(opened, range(0, C, P)):
             expert_pass(bank[:], E - 1, c0, 0)
-        gb = interleave_second(1)
-        quantize_slots(1, 0, ga)
-        expert(0)
-        expert(1)
-        ga = interleave_second(2)
-        quantize_slots(1, 1, gb)
-        expert(2)
-        expert(3)
-        gb = interleave_second(3)
-        quantize_slots(1, 2, ga)
-        expert(4)
-        expert(5)
-        ga = interleave_second(4)
-        quantize_slots(1, 3, gb)
-        expert(6)
-        quantize_slots(1, 4, ga)
+        for i, (s0, s1) in enumerate(SLOT_CHUNKS[1][:-1]):
+            following = interleave_second(i + 1)
+            quantize_slots(1, i, grouped)
+            for expert_index in range(s0 // C, s1 // C):
+                expert(expert_index)
+            grouped = following
+        quantize_slots(1, len(SLOT_CHUNKS[1]) - 1, grouped)
         for bank, c0 in zip(opened, range(0, C, P)):
             expert_pass(bank[:], E - 1, c0, 1)
-            s0 = (E - 1) * C + c0
-            nc.scalar.activation(out=y[:, s0:s0 + P], in_=bank[:], func=IDENTITY, bias=bias[:, E - 1:E])
+            add_bias(bank[:], E - 1, c0, c0 + P)
 
-        def weigh(dst, pos_sb, g, t0, t1):
+        def weigh(dst, pos_sb, choice, t0, t1):
             nc.vector.tensor_tensor(
                 out=dst[:, t0:t1],
                 in0=y[:].indirect(pos_sb[:, t0 // LIST_ROWS:t1 // LIST_ROWS]),
-                in1=gates[:, g, t0:t1],
+                in1=gates[:, choice, t0:t1],
                 op=MULT,
             )
 

@@ -46,7 +46,7 @@ TOKEN_LOADS = [(f, t0, t1) for t0, t1 in TOKEN_GROUPS for f in range(PASSES)][:-
 FIRST_GATHERS = spans([768, 512, 768])
 SECOND_GATHERS = spans([768, 768, 512])
 SLOT_CHUNKS = (spans([512, 512, 512, 512]), spans([512, 512, 512, 256, 256]))
-OUT_CHUNKS = spans([512, 384, 128])
+OUT_CHUNKS = spans([320, 256, 256, 128, 64])
 
 
 def tile_moe_prv_lin_bias_kernel(
@@ -81,8 +81,7 @@ def tile_moe_prv_lin_bias_kernel(
         s_codes = keep.tile([P, PASSES, S], U32, name="s_codes", align_bytes=64)
         s_plane = keep.tile([P, PASSES, S], U8, name="s_plane", align_bytes=64)
         y = keep.tile([P, S], F32, name="y")
-        first = keep.tile([P, T], F32, name="first")
-        second = keep.tile([P, T], F32, name="second")
+        weighed = keep.tile([P, 2, T], F32, name="weighed")
         total = keep.tile([P, T], F32, name="total")
 
         nc.vector.memset(w_plane[:].rearrange("p g n -> p (g n)").bitcast(I32), 0)
@@ -307,21 +306,26 @@ def tile_moe_prv_lin_bias_kernel(
             expert_pass(bank[:], E - 1, c0, 1)
             add_bias(bank[:], E - 1, c0, c0 + P)
 
-        def weigh(dst, pos_sb, choice, t0, t1):
-            nc.vector.tensor_tensor(
-                out=dst[:, t0:t1],
-                in0=y[:].indirect(pos_sb[:, t0 // LIST_ROWS:t1 // LIST_ROWS]),
-                in1=gates[:, choice, t0:t1],
-                op=MULT,
-            )
+        def positions(pos_sb, t0, t1):
+            return y[:].indirect(pos_sb[:, t0 // LIST_ROWS:t1 // LIST_ROWS])
 
         def finish(t0, t1):
-            nc.vector.tensor_tensor(out=total[:, t0:t1], in0=first[:, t0:t1], in1=second[:, t0:t1], op=ADD)
+            nc.vector.tensor_tensor(out=total[:, t0:t1], in0=weighed[:, 0, t0:t1], in1=weighed[:, 1, t0:t1], op=ADD)
             nc.sync.dma_start(out=out[:, t0:t1], in_=total[:, t0:t1])
 
         for i, (t0, t1) in enumerate(OUT_CHUNKS):
-            weigh(first, pos1_sb, 0, t0, t1)
-            weigh(second, pos2_sb, 1, t0, t1)
-            if i > 0:
-                finish(*OUT_CHUNKS[i - 1])
+            if i == 0:
+                for choice, pos_sb in enumerate((pos1_sb, pos2_sb)):
+                    nc.vector.tensor_tensor(
+                        out=weighed[:, choice, t0:t1],
+                        in0=positions(pos_sb, t0, t1),
+                        in1=gates[:, choice, t0:t1],
+                        op=MULT,
+                    )
+                continue
+            fetched = keep.tile([P, 2, t1 - t0], F32, name=f"fetched{i}")
+            for choice, pos_sb in enumerate((pos1_sb, pos2_sb)):
+                nc.scalar.activation(out=fetched[:, choice, :], in_=positions(pos_sb, t0, t1), func=COPY)
+            nc.vector.tensor_tensor(out=weighed[:, :, t0:t1], in0=fetched[:], in1=gates[:, :, t0:t1], op=MULT)
+            finish(*OUT_CHUNKS[i - 1])
         finish(*OUT_CHUNKS[-1])

@@ -39,10 +39,8 @@ def spans(widths):
 
 
 TOKEN_GROUPS = spans([GROUP] * (T // GROUP))
-TOKEN_LOADS = [(f, t0, t1) for t0, t1 in TOKEN_GROUPS for f in range(PASSES)][:-1] + [
-    (1, T - GROUP, T - GROUP // 2),
-    (1, T - GROUP // 2, T),
-]
+LATE_LOADS = spans([512, 256, 128, 128])
+FIRST_BANKS = (spans([256, 256, 256, 128, 128]), TOKEN_GROUPS)
 FIRST_GATHERS = spans([768, 512, 768])
 SECOND_GATHERS = spans([768, 768, 512])
 SLOT_CHUNKS = (spans([512, 512, 512, 512]), spans([512, 512, 512, 256, 256]))
@@ -69,11 +67,12 @@ def tile_moe_prv_lin_bias_kernel(
             [keep.tile([P, PACK, PASS], F32, name=f"wu_raw{a}{f}", align_bytes=64) for f in range(PASSES)]
             for a in range(PASSES)
         ]
-        u_raw = [keep.tile([P, PACK, t1 - t0], F32, name=f"u_raw{i}") for i, (f, t0, t1) in enumerate(TOKEN_LOADS)]
+        u_early = keep.tile([P, PACK, T], F32, name="u_early")
+        u_late = [keep.tile([P, PACK, t1 - t0], F32, name=f"u_late{i}") for i, (t0, t1) in enumerate(LATE_LOADS)]
         wu_codes = keep.tile([P, PASSES, PASSES, PASS], U32, name="wu_codes", align_bytes=64)
         wu_plane = keep.tile([P, PASSES, PASSES, PASS], U8, name="wu_plane", align_bytes=64)
-        u_codes = keep.tile([P, PASSES * T], U32, name="u_codes", align_bytes=64)
-        u_plane = keep.tile([P, PASSES * T], U8, name="u_plane", align_bytes=64)
+        u_codes = keep.tile([P, PASSES, T], U32, name="u_codes", align_bytes=64)
+        u_plane = keep.tile([P, PASSES, T], U8, name="u_plane", align_bytes=64)
         x_pairs = {(a, h): keep.tile([P, T], U32, name=f"x_pairs{a}{h}", align_bytes=64) for a, h in ((0, 0), (0, 1), (1, 0))}
         x_rows = keep.tile([P, 2, T], BF16, name="x_rows", align_bytes=64)
         picked_first = {}
@@ -90,16 +89,15 @@ def tile_moe_prv_lin_bias_kernel(
             rows = wu[f * PASS:(f + 1) * PASS, a * PASS:(a + 1) * PASS]
             nc.sync.dma_start(out=wu_raw[a][f][:], in_=rows.rearrange("(p j) c -> p j c", j=PACK))
 
-        def load_u(i):
-            f, t0, t1 = TOKEN_LOADS[i]
+        def load_u(raw, f, t0, t1):
             rows = uT[f * PASS:(f + 1) * PASS, t0:t1]
-            nc.sync.dma_start(out=u_raw[i][:], in_=rows.rearrange("(p j) t -> p j t", j=PACK))
+            nc.sync.dma_start(out=raw[:], in_=rows.rearrange("(p j) t -> p j t", j=PACK))
 
-        load_u(0)
-        for f in range(PASSES):
-            load_wu(0, f)
-        for i in range(1, len(TOKEN_LOADS)):
-            load_u(i)
+        load_wu(0, 0)
+        load_u(u_early, 0, 0, T)
+        load_wu(0, 1)
+        for raw, (t0, t1) in zip(u_late, LATE_LOADS):
+            load_u(raw, 1, t0, t1)
         nc.sync.dma_start(offs_sb[:], offs)
         for f in range(PASSES):
             load_wu(1, f)
@@ -130,55 +128,46 @@ def tile_moe_prv_lin_bias_kernel(
         def quantize_wu(a, f, grouped):
             nc.vector.quantize_mx(out=wu_codes[:, a, f, :].bitcast(FP8X4), scales=wu_plane[:, a, f, :], in_=grouped[:])
 
-        def u_columns(f, t0, width):
-            start = PASSES * GROUP * (t0 // GROUP) + f * GROUP + t0 % GROUP
-            return slice(start, start + width)
-
-        def round_u(i, copy, grouped):
-            copy(
-                out=grouped.rearrange("p (c i j) -> p c j i", i=RUN, j=PACK),
-                in_=u_raw[i][:].rearrange("p j (c i) -> p c j i", i=RUN),
-            )
-
-        def round_loads(i, copies):
-            widths = [PACK * (t1 - t0) for f, t0, t1 in TOKEN_LOADS[i:i + len(copies)]]
-            grouped = stage.tile([P, sum(widths)], BF16, name="narrow", align_bytes=64)
-            for n, (copy, (x0, x1)) in enumerate(zip(copies, spans(widths))):
-                round_u(i + n, copy, grouped[:, x0:x1])
+        def round_u(raw, shares):
+            grouped = stage.tile([P, PACK * raw.shape[2]], BF16, name="narrow", align_bytes=64)
+            for copy, (t0, t1) in zip([c for c, w in shares], spans([w for c, w in shares])):
+                copy(
+                    out=grouped[:, PACK * t0:PACK * t1].rearrange("p (c i j) -> p c j i", i=RUN, j=PACK),
+                    in_=raw[:, :, t0:t1].rearrange("p j (c i) -> p c j i", i=RUN),
+                )
             return grouped
 
-        def quantize_u(i, grouped):
-            f, t0, t1 = TOKEN_LOADS[i]
-            cols = u_columns(f, t0, grouped.shape[1] // PACK)
-            nc.vector.quantize_mx(out=u_codes[:, cols].bitcast(FP8X4), scales=u_plane[:, cols], in_=grouped[:])
+        def quantize_u(f, t0, t1, grouped):
+            nc.vector.quantize_mx(out=u_codes[:, f, t0:t1].bitcast(FP8X4), scales=u_plane[:, f, t0:t1], in_=grouped[:])
 
-        def project_pass(bank, a, h, e, f, t0, t1):
+        def project_pass(bank, a, h, e, f, t0, t1, start, stop):
             cols = slice((2 * h + e) * P, (2 * h + e + 1) * P)
             nc.tensor.matmul_mx(
                 out=bank[:, e, :],
                 lhsT=wu_codes[:, a, f, cols].bitcast(FP8X4),
                 lhsT_scale=wu_plane[:, a, f, cols],
-                rhs=u_codes[:, u_columns(f, t0, t1 - t0)].bitcast(FP8X4),
-                rhs_scale=u_plane[:, u_columns(f, t0, t1 - t0)],
-                start=(f == 0),
-                stop=(f == PASSES - 1),
+                rhs=u_codes[:, f, t0:t1].bitcast(FP8X4),
+                rhs_scale=u_plane[:, f, t0:t1],
+                start=start,
+                stop=stop,
             )
 
         def open_bank(a, h, t0, t1):
             bank = psum.tile([P, 2, t1 - t0], F32, name="bank")
-            project_pass(bank, a, h, 0, 0, t0, t1)
+            for e in range(2):
+                project_pass(bank, a, h, e, 0, t0, t1, e == 0, False)
             return bank
 
-        def close_bank(bank, a, h, t0, t1):
-            for e, f in ((0, 1), (1, 0), (1, 1)):
-                project_pass(bank, a, h, e, f, t0, t1)
+        def close_bank(bank, a, h, t0, t1, copy=on_scalar):
+            for e in range(2):
+                project_pass(bank, a, h, e, 1, t0, t1, False, e == 1)
             if (a, h) in x_pairs:
-                nc.scalar.copy(
+                copy(
                     out=x_pairs[a, h][:, t0:t1].bitcast(BF16).rearrange("p (t e) -> p t e", e=2),
                     in_=bank[:].rearrange("p e t -> p t e"),
                 )
             else:
-                nc.scalar.copy(out=x_rows[:, :, t0:t1], in_=bank[:])
+                copy(out=x_rows[:, :, t0:t1], in_=bank[:])
 
         def project(a, h, t0, t1):
             close_bank(open_bank(a, h, t0, t1), a, h, t0, t1)
@@ -250,23 +239,37 @@ def tile_moe_prv_lin_bias_kernel(
             add_bias(bank[:], expert_index, 0, C)
 
         halves = [(on_scalar, slice(0, 2)), (on_vector, slice(2, PACK))]
-        quantize_u(0, round_loads(0, [on_vector]))
         quantize_wu(0, 0, round_wu(0, 0, halves))
-        weights = round_wu(0, 1, halves)
-        tokens = round_loads(1, [on_vector])
-        quantize_wu(0, 1, weights)
-        quantize_u(1, tokens)
-        for h in range(2):
-            project(0, h, *TOKEN_GROUPS[0])
-        for g, copies in ((1, [on_scalar, on_vector]), (2, [on_vector, on_vector])):
-            quantize_u(PASSES * g, round_loads(PASSES * g, copies))
-            for h in range(2):
-                project(0, h, *TOKEN_GROUPS[g])
-        for i in range(PASSES * (len(TOKEN_GROUPS) - 1), len(TOKEN_LOADS)):
-            f, t0, t1 = TOKEN_LOADS[i]
-            quantize_u(i, round_loads(i, [on_vector]))
-            if f == PASSES - 1:
-                project(0, 0, t0, t1)
+        early = [round_u(u_early[:, :, t0:t1], [(on_scalar, 192), (on_vector, 320)]) for t0, t1 in spans([T // 2] * 2)]
+        for grouped, (t0, t1) in zip(early, spans([T // 2] * 2)):
+            quantize_u(0, t0, t1, grouped)
+        banks = {(h, t0): open_bank(0, h, t0, t1) for h in range(2) for t0, t1 in FIRST_BANKS[h][:5 - 2 * h]}
+        quantize_wu(0, 1, round_wu(0, 1, halves))
+
+        def close_first(h, i, copy=on_scalar):
+            t0, t1 = FIRST_BANKS[h][i]
+            close_bank(banks[h, t0], 0, h, t0, t1, copy)
+
+        ranges = FIRST_BANKS[0]
+        late = [
+            round_u(u_late[0][:, :, :GROUP], [(on_vector, GROUP)]),
+            round_u(u_late[0][:, :, GROUP:], [(on_scalar, GROUP)]),
+        ]
+        quantize_u(1, *ranges[0], late[0])
+        close_first(0, 0)
+        late.append(round_u(u_late[1][:], [(on_vector, GROUP)]))
+        quantize_u(1, *ranges[1], late[1])
+        close_first(0, 1)
+        close_first(1, 0)
+        quantize_u(1, *ranges[2], late[2])
+        close_first(0, 2)
+        late.extend(round_u(raw[:], [(on_vector, GROUP // 2)]) for raw in u_late[2:])
+        quantize_u(1, *ranges[3], late[3])
+        close_first(0, 3)
+        quantize_u(1, *ranges[4], late[4])
+        close_first(1, 1, on_vector)
+        close_first(0, 4, on_vector)
+        close_first(1, 2)
         project(0, 1, *TOKEN_GROUPS[-1])
 
         late = [round_wu(1, f, [(on_scalar, slice(0, PACK))]) for f in range(PASSES)]

@@ -41,9 +41,9 @@ def spans(widths):
 TOKEN_GROUPS = spans([GROUP] * (T // GROUP))
 LATE_LOADS = spans([512, 256, 128, 128])
 FIRST_BANKS = (spans([256, 256, 256, 128, 128]), TOKEN_GROUPS)
-FIRST_GATHERS = spans([768, 512, 768])
-SECOND_GATHERS = spans([768, 768, 512])
-SLOT_CHUNKS = (spans([512, 512, 512, 512]), spans([512, 512, 512, 256, 256]))
+FIRST_CHUNKS = spans([640, 768, 640])
+CHUNK = 512
+SECOND_CHUNKS = spans([CHUNK] * (S // CHUNK))
 OUT_CHUNKS = spans([320, 256, 256, 128, 64])
 
 
@@ -63,20 +63,19 @@ def tile_moe_prv_lin_bias_kernel(
         gates = keep.tile([P, 2, T], F32, name="gates")
         w_codes = keep.tile([P, E * PASSES, 2 * N], U8, name="w_codes", align_bytes=64)
         w_plane = keep.tile([P, E * PASSES, N], U8, name="w_plane", align_bytes=64)
-        wu_raw = [
-            [keep.tile([P, PACK, PASS], F32, name=f"wu_raw{a}{f}", align_bytes=64) for f in range(PASSES)]
+        wu_raw = {
+            (a, f): keep.tile([P, PACK, PASS], F32, name=f"wu_raw{a}{f}", align_bytes=64)[:]
             for a in range(PASSES)
-        ]
+            for f in range(PASSES)
+        }
+        arena = keep.tile([P, 5120], U32, name="arena", align_bytes=64)
         u_early = keep.tile([P, PACK, T], F32, name="u_early")
         u_late = [keep.tile([P, PACK, t1 - t0], F32, name=f"u_late{i}") for i, (t0, t1) in enumerate(LATE_LOADS)]
-        wu_codes = keep.tile([P, PASSES, PASSES, PASS], U32, name="wu_codes", align_bytes=64)
-        wu_plane = keep.tile([P, PASSES, PASSES, PASS], U8, name="wu_plane", align_bytes=64)
+        wu_codes = {}
         u_codes = keep.tile([P, PASSES, T], U32, name="u_codes", align_bytes=64)
         u_plane = keep.tile([P, PASSES, T], U8, name="u_plane", align_bytes=64)
         x_pairs = {(a, h): keep.tile([P, T], U32, name=f"x_pairs{a}{h}", align_bytes=64) for a, h in ((0, 0), (0, 1), (1, 0))}
         x_rows = keep.tile([P, 2, T], BF16, name="x_rows", align_bytes=64)
-        picked_first = {}
-        picked_second = keep.tile([P, 2, S], U32, name="picked_second", align_bytes=64)
         s_codes = keep.tile([P, PASSES, S], U32, name="s_codes", align_bytes=64)
         s_plane = keep.tile([P, PASSES, S], U8, name="s_plane", align_bytes=64)
         y = keep.tile([P, S], F32, name="y")
@@ -87,7 +86,7 @@ def tile_moe_prv_lin_bias_kernel(
 
         def load_wu(a, f):
             rows = wu[f * PASS:(f + 1) * PASS, a * PASS:(a + 1) * PASS]
-            nc.sync.dma_start(out=wu_raw[a][f][:], in_=rows.rearrange("(p j) c -> p j c", j=PACK))
+            nc.sync.dma_start(out=wu_raw[a, f], in_=rows.rearrange("(p j) c -> p j c", j=PACK))
 
         def load_u(raw, f, t0, t1):
             rows = uT[f * PASS:(f + 1) * PASS, t0:t1]
@@ -117,16 +116,27 @@ def tile_moe_prv_lin_bias_kernel(
         on_vector = nc.vector.tensor_copy
         on_scalar = nc.scalar.copy
 
-        def round_wu(a, f, shares):
-            grouped = keep.tile([P, PACK * PASS], BF16, name=f"shared{PASSES * a + f}", align_bytes=64)
-            dst = grouped[:].rearrange("p (d m j) -> p m j d", d=PACK, j=PACK)
-            src = wu_raw[a][f][:].rearrange("p j (m d) -> p m j d", d=PACK)
-            for copy, ds in shares:
-                copy(out=dst[:, :, :, ds], in_=src[:, :, :, ds])
-            return grouped
+        def round_wu(a, f, h, copy, grouped):
+            copy(
+                out=grouped.rearrange("p (e m j) -> p m j e", e=2, j=PACK),
+                in_=wu_raw[a, f].rearrange("p j (m d) -> p m j d", d=PACK)[:, :, :, 2 * h:2 * h + 2],
+            )
 
-        def quantize_wu(a, f, grouped):
-            nc.vector.quantize_mx(out=wu_codes[:, a, f, :].bitcast(FP8X4), scales=wu_plane[:, a, f, :], in_=grouped[:])
+        def round_two(parts, grouped):
+            for (a, f, h, copy), (x0, x1) in zip(parts, spans([2 * PASS] * 2)):
+                round_wu(a, f, h, copy, grouped[:, x0:x1])
+            return [part[:3] for part in parts], grouped
+
+        def rounded_tile(name):
+            return keep.tile([P, PACK * PASS], BF16, name=name, align_bytes=64)[:]
+
+        def quantize_wu(keys, grouped):
+            name = "%d%d%d" % keys[0]
+            codes = keep.tile([P, PASS], U32, name="wu_codes" + name, align_bytes=64)
+            plane = keep.tile([P, PASS], U8, name="wu_plane" + name, align_bytes=64)
+            nc.vector.quantize_mx(out=codes[:].bitcast(FP8X4), scales=plane[:], in_=grouped)
+            for key, (x0, x1) in zip(keys, spans([2 * P] * 2)):
+                wu_codes[key] = (codes[:, x0:x1], plane[:, x0:x1])
 
         def round_u(raw, shares):
             grouped = stage.tile([P, PACK * raw.shape[2]], BF16, name="narrow", align_bytes=64)
@@ -141,11 +151,12 @@ def tile_moe_prv_lin_bias_kernel(
             nc.vector.quantize_mx(out=u_codes[:, f, t0:t1].bitcast(FP8X4), scales=u_plane[:, f, t0:t1], in_=grouped[:])
 
         def project_pass(bank, a, h, e, f, t0, t1, start, stop):
-            cols = slice((2 * h + e) * P, (2 * h + e + 1) * P)
+            codes, plane = wu_codes[a, f, h]
+            cols = slice(e * P, (e + 1) * P)
             nc.tensor.matmul_mx(
                 out=bank[:, e, :],
-                lhsT=wu_codes[:, a, f, cols].bitcast(FP8X4),
-                lhsT_scale=wu_plane[:, a, f, cols],
+                lhsT=codes[:, cols].bitcast(FP8X4),
+                lhsT_scale=plane[:, cols],
                 rhs=u_codes[:, f, t0:t1].bitcast(FP8X4),
                 rhs_scale=u_plane[:, f, t0:t1],
                 start=start,
@@ -178,73 +189,57 @@ def tile_moe_prv_lin_bias_kernel(
         def gather(dst, a, h, s0, s1):
             nc.vector.tensor_copy(out=dst, in_=x_pairs[a, h][:].indirect(offsets(s0, s1)))
 
-        def gather_first(i, buffer):
-            s0, s1 = FIRST_GATHERS[i]
-            picked_first[i] = keep.tile([P, 2, s1 - s0], U32, name=buffer, align_bytes=64)
-            for h in range(2):
-                gather(picked_first[i][:, h, :], 0, h, s0, s1)
-
-        def gather_rows(c0):
-            halves = picked_second[:, 1, c0:c0 + C].bitcast(BF16).rearrange("p (s e) -> p e s", e=2)
+        def gather_rows(dst, s0, s1):
+            halves = dst.bitcast(BF16).rearrange("p (s e) -> p e s", e=2)
             for e in range(2):
-                nc.scalar.activation(out=halves[:, e, :], in_=x_rows[:, e, :].indirect(offsets(c0, c0 + C)), func=COPY)
+                nc.scalar.activation(out=halves[:, e, :], in_=x_rows[:, e, :].indirect(offsets(s0, s1)), func=COPY)
 
-        def interleave(copy, grouped, pairs):
+        def interleave(copy, word, woven, pairs):
             copy(
-                out=grouped.bitcast(F32).rearrange("p (s h) -> p s h", h=2),
-                in_=pairs.bitcast(F32).rearrange("p h s -> p s h"),
+                out=woven.bitcast(word).rearrange("p (s h) -> p s h", h=2),
+                in_=pairs.bitcast(word).rearrange("p h s -> p s h"),
             )
+            return woven
 
-        def interleave_first(i, copy):
-            s0, s1 = FIRST_GATHERS[i]
-            interleave(copy, first_grouped[:, PACK * s0:PACK * s1], picked_first[i][:])
+        def quantize_slots(a, s0, woven, widths):
+            for x0, x1 in spans(widths):
+                nc.vector.quantize_mx(
+                    out=s_codes[:, a, s0 + x0:s0 + x1].bitcast(FP8X4),
+                    scales=s_plane[:, a, s0 + x0:s0 + x1],
+                    in_=woven[:, 2 * x0:2 * x1].bitcast(BF16),
+                )
 
-        def interleave_second(i):
-            s0, s1 = SLOT_CHUNKS[1][i]
-            grouped = stage.tile([P, PACK * (s1 - s0)], BF16, name="wide", align_bytes=64)
-            interleave(on_vector, grouped[:], picked_second[:, :, s0:s1])
-            return grouped[:]
-
-        def quantize_slots(a, i, grouped):
-            s0, s1 = SLOT_CHUNKS[a][i]
-            nc.vector.quantize_mx(out=s_codes[:, a, s0:s1].bitcast(FP8X4), scales=s_plane[:, a, s0:s1], in_=grouped)
-
-        def quantize_first(i):
-            s0, s1 = SLOT_CHUNKS[0][i]
-            quantize_slots(0, i, first_grouped[:, PACK * s0:PACK * s1])
-
-        def expert_pass(sums, expert_index, c0, a):
-            slots = slice(expert_index * C + c0, expert_index * C + c0 + P)
+        def expert_pass(bank, expert_index, s0, s1, a):
             nc.tensor.matmul_mx(
-                out=sums,
+                out=bank[:],
                 lhsT=w_codes[:, expert_index * PASSES + a, :].bitcast(FP4X4),
                 lhsT_scale=w_plane[:, expert_index * PASSES + a, :],
-                rhs=s_codes[:, a, slots].bitcast(FP8X4),
-                rhs_scale=s_plane[:, a, slots],
+                rhs=s_codes[:, a, s0:s1].bitcast(FP8X4),
+                rhs_scale=s_plane[:, a, s0:s1],
                 start=(a == 0),
                 stop=(a == PASSES - 1),
             )
 
-        def add_bias(sums, expert_index, c0, c1):
-            s0 = expert_index * C
-            nc.scalar.activation(
-                out=y[:, s0 + c0:s0 + c1], in_=sums, func=IDENTITY, bias=bias[:, expert_index:expert_index + 1]
-            )
+        def add_bias(bank, expert_index, s0, s1, on_vector_engine=False):
+            column = bias[:, expert_index:expert_index + 1]
+            if on_vector_engine:
+                nc.vector.tensor_scalar(out=y[:, s0:s1], in0=bank[:], scalar1=column, scalar2=None, op0=ADD)
+            else:
+                nc.scalar.activation(out=y[:, s0:s1], in_=bank[:], func=IDENTITY, bias=column)
 
-        def expert(expert_index):
+        def expert(expert_index, on_vector_engine=False):
+            s0, s1 = expert_index * C, (expert_index + 1) * C
             bank = psum.tile([P, C], F32, name="bank")
-            for c0 in range(0, C, P):
-                for a in range(PASSES):
-                    expert_pass(bank[:, c0:c0 + P], expert_index, c0, a)
-            add_bias(bank[:], expert_index, 0, C)
+            for a in range(PASSES):
+                expert_pass(bank, expert_index, s0, s1, a)
+            add_bias(bank, expert_index, s0, s1, on_vector_engine)
 
-        halves = [(on_scalar, slice(0, 2)), (on_vector, slice(2, PACK))]
-        quantize_wu(0, 0, round_wu(0, 0, halves))
+        quantize_wu(*round_two([(0, 0, 0, on_scalar), (0, 0, 1, on_vector)], rounded_tile("rounded0")))
         early = [round_u(u_early[:, :, t0:t1], [(on_scalar, 192), (on_vector, 320)]) for t0, t1 in spans([T // 2] * 2)]
         for grouped, (t0, t1) in zip(early, spans([T // 2] * 2)):
             quantize_u(0, t0, t1, grouped)
         banks = {(h, t0): open_bank(0, h, t0, t1) for h in range(2) for t0, t1 in FIRST_BANKS[h][:5 - 2 * h]}
-        quantize_wu(0, 1, round_wu(0, 1, halves))
+        quantize_wu(*round_two([(0, 1, 0, on_scalar), (0, 1, 1, on_vector)], rounded_tile("rounded1")))
 
         def close_first(h, i, copy=on_scalar):
             t0, t1 = FIRST_BANKS[h][i]
@@ -272,42 +267,80 @@ def tile_moe_prv_lin_bias_kernel(
         close_first(1, 2)
         project(0, 1, *TOKEN_GROUPS[-1])
 
-        late = [round_wu(1, f, [(on_scalar, slice(0, PACK))]) for f in range(PASSES)]
-        gather_first(0, "shared0")
-        quantize_wu(1, 0, late[0])
-        banks = {(h, t0, t1): open_bank(1, h, t0, t1) for h in range(2) for t0, t1 in TOKEN_GROUPS}
-        gather_first(1, "shared2")
-        quantize_wu(1, 1, late[1])
-        first_grouped = keep.tile([P, PACK * S], BF16, name="wu_raw11", align_bytes=64)
-        for (h, t0, t1), bank in banks.items():
-            close_bank(bank, 1, h, t0, t1)
-        gather_first(2, "shared3")
-        interleave_first(0, on_scalar)
-        interleave_first(1, on_vector)
-        quantize_first(0)
-        interleave_first(2, on_vector)
-        quantize_first(1)
+        on_gpsimd = nc.gpsimd.tensor_copy
 
-        for s0, s1 in SECOND_GATHERS:
-            gather(picked_second[:, 0, s0:s1], 1, 0, s0, s1)
-        for c0 in range(0, S, C):
-            gather_rows(c0)
-        quantize_first(2)
-        grouped = interleave_second(0)
-        quantize_first(3)
+        def pairs_at(start, slots):
+            return arena[:, start:start + 2 * slots].rearrange("p (h s) -> p h s", h=2)
+
+        first_pairs = [pairs_at(0, 640), pairs_at(3072, 768), pairs_at(0, 640)]
+        first_woven = arena[:, 1536:3072]
+        second_pairs = [pairs_at(4096, CHUNK), pairs_at(3072, CHUNK), pairs_at(0, CHUNK), pairs_at(4096, CHUNK)]
+        second_woven = keep.tile([P, 2 * CHUNK], U32, name="second_woven", align_bytes=64)[:]
+
+        def gather_first(c):
+            for h in range(2):
+                gather(first_pairs[c][:, h, :], 0, h, *FIRST_CHUNKS[c])
+
+        def weave_first(c):
+            s0, s1 = FIRST_CHUNKS[c]
+            interleave(on_gpsimd, U32, first_woven[:, :2 * (s1 - s0)], first_pairs[c])
+
+        def gather_second(c):
+            gather(second_pairs[c][:, 0, :], 1, 0, *SECOND_CHUNKS[c])
+
+        gather_first(0)
+        late = [
+            round_two([(1, 0, h, on_scalar), (1, 1, h, copy)], arena[:, x0:x0 + 1024].bitcast(BF16))
+            for h, x0, copy in ((1, 2304, on_vector), (0, 4096, on_scalar))
+        ]
+        quantize_wu(*late[0])
+        for t0, t1 in TOKEN_GROUPS:
+            project(1, 1, t0, t1)
+        gather(first_pairs[1][:, 0, :], 0, 0, *FIRST_CHUNKS[1])
+        weave_first(0)
+        quantize_wu(*late[1])
+        for t0, t1 in TOKEN_GROUPS:
+            project(1, 0, t0, t1)
+        gather(first_pairs[1][:, 1, :], 0, 1, *FIRST_CHUNKS[1])
+        quantize_slots(0, 0, first_woven, [512, 128])
+        gather_first(2)
+        weave_first(1)
+        gather_rows(second_pairs[0][:, 1, :], *SECOND_CHUNKS[0])
+        quantize_slots(0, 640, first_woven, [512, 256])
+        gather_second(0)
+        gather_second(1)
+        gather_rows(second_pairs[1][:, 1, :], *SECOND_CHUNKS[1])
+        weave_first(2)
+        gather_second(2)
+        gather_rows(second_pairs[2][:, 1, :], *SECOND_CHUNKS[2])
+        interleave(on_gpsimd, U32, second_woven, second_pairs[0])
+        quantize_slots(0, 1408, first_woven, [512, 128])
+        quantize_slots(1, 0, second_woven, [512])
+        gather_second(3)
+        expert(0, True)
+        expert(1, True)
+        interleave(on_gpsimd, U32, second_woven, second_pairs[1])
+        for x0, x1 in spans([C, C]):
+            gather_rows(second_pairs[3][:, 1, x0:x1], 1536 + x0, 1536 + x1)
+        quantize_slots(1, 512, second_woven, [512])
+        expert(2)
+        expert(3)
+        last_woven = keep.tile([P, 4 * CHUNK], U32, name="x_pairs10", align_bytes=64)
+        interleave(on_vector, F32, last_woven[:, :1024], second_pairs[2])
         opened = [psum.tile([P, P], F32, name="bank") for c0 in range(0, C, P)]
-        for bank, c0 in zip(opened, range(0, C, P)):
-            expert_pass(bank[:], E - 1, c0, 0)
-        for i, (s0, s1) in enumerate(SLOT_CHUNKS[1][:-1]):
-            following = interleave_second(i + 1)
-            quantize_slots(1, i, grouped)
-            for expert_index in range(s0 // C, s1 // C):
-                expert(expert_index)
-            grouped = following
-        quantize_slots(1, len(SLOT_CHUNKS[1]) - 1, grouped)
-        for bank, c0 in zip(opened, range(0, C, P)):
-            expert_pass(bank[:], E - 1, c0, 1)
-            add_bias(bank[:], E - 1, c0, c0 + P)
+        for bank, (s0, s1) in zip(opened, spans([S - C, P, P])[1:]):
+            expert_pass(bank, E - 1, s0, s1, 0)
+        interleave(on_vector, F32, last_woven[:, 1024:1536], second_pairs[3][:, :, :C])
+        quantize_slots(1, 1024, last_woven, [512])
+        expert(4)
+        expert(5)
+        interleave(on_vector, F32, last_woven[:, 1536:], second_pairs[3][:, :, C:])
+        quantize_slots(1, 1536, last_woven[:, 1024:], [256])
+        expert(6)
+        quantize_slots(1, 1792, last_woven[:, 1536:], [256])
+        for bank, (s0, s1) in zip(opened, spans([S - C, P, P])[1:]):
+            expert_pass(bank, E - 1, s0, s1, 1)
+            add_bias(bank, E - 1, s0, s1)
 
         def positions(pos_sb, t0, t1):
             return y[:].indirect(pos_sb[:, t0 // LIST_ROWS:t1 // LIST_ROWS])

@@ -41,7 +41,7 @@ def spans(widths):
 TOKEN_GROUPS = spans([GROUP] * (T // GROUP))
 LATE_LOADS = spans([512, 256, 128, 128])
 FIRST_BANKS = (spans([256, 256, 256, 128, 128]), TOKEN_GROUPS)
-FIRST_CHUNKS = spans([640, 768, 640])
+FIRST_CHUNKS = spans([768, 768, 512])
 CHUNK = 512
 SECOND_CHUNKS = spans([CHUNK] * (S // CHUNK))
 OUT_CHUNKS = spans([320, 256, 256, 128, 64])
@@ -68,7 +68,7 @@ def tile_moe_prv_lin_bias_kernel(
             for a in range(PASSES)
             for f in range(PASSES)
         }
-        arena = keep.tile([P, 5120], U32, name="arena", align_bytes=64)
+        arena = keep.tile([P, 5632], U32, name="arena", align_bytes=64)
         u_early = keep.tile([P, PACK, T], F32, name="u_early")
         u_late = [keep.tile([P, PACK, t1 - t0], F32, name=f"u_late{i}") for i, (t0, t1) in enumerate(LATE_LOADS)]
         wu_codes = {}
@@ -76,7 +76,7 @@ def tile_moe_prv_lin_bias_kernel(
         u_plane = keep.tile([P, PASSES, T], U8, name="u_plane", align_bytes=64)
         x_pairs = {(a, h): keep.tile([P, T], U32, name=f"x_pairs{a}{h}", align_bytes=64) for a, h in ((0, 0), (0, 1), (1, 0))}
         x_rows = keep.tile([P, 2, T], BF16, name="x_rows", align_bytes=64)
-        s_codes = keep.tile([P, PASSES, S], U32, name="s_codes", align_bytes=64)
+        s_codes = {(a, 0): keep.tile([P, S], U32, name=f"s_codes{a}", align_bytes=64) for a in range(PASSES)}
         s_plane = keep.tile([P, PASSES, S], U8, name="s_plane", align_bytes=64)
         y = keep.tile([P, S], F32, name="y")
         weighed = keep.tile([P, 2, T], F32, name="weighed")
@@ -116,10 +116,11 @@ def tile_moe_prv_lin_bias_kernel(
         on_vector = nc.vector.tensor_copy
         on_scalar = nc.scalar.copy
 
-        def round_wu(a, f, h, copy, grouped):
+        def round_wu(a, f, h, copy, grouped, order="p m j e"):
+            columns = wu_raw[a, f].rearrange("p j (m h e) -> p j m h e", h=2, e=2)[:, :, :, h, :]
             copy(
-                out=grouped.rearrange("p (e m j) -> p m j e", e=2, j=PACK),
-                in_=wu_raw[a, f].rearrange("p j (m d) -> p m j d", d=PACK)[:, :, :, 2 * h:2 * h + 2],
+                out=grouped.rearrange("p (e m j) -> " + order, e=2, j=PACK),
+                in_=columns.rearrange("p j m e -> " + order),
             )
 
         def round_two(parts, grouped):
@@ -132,10 +133,10 @@ def tile_moe_prv_lin_bias_kernel(
 
         def quantize_wu(keys, grouped):
             name = "%d%d%d" % keys[0]
-            codes = keep.tile([P, PASS], U32, name="wu_codes" + name, align_bytes=64)
-            plane = keep.tile([P, PASS], U8, name="wu_plane" + name, align_bytes=64)
+            codes = keep.tile([P, 2 * P * len(keys)], U32, name="wu_codes" + name, align_bytes=64)
+            plane = keep.tile([P, 2 * P * len(keys)], U8, name="wu_plane" + name, align_bytes=64)
             nc.vector.quantize_mx(out=codes[:].bitcast(FP8X4), scales=plane[:], in_=grouped)
-            for key, (x0, x1) in zip(keys, spans([2 * P] * 2)):
+            for key, (x0, x1) in zip(keys, spans([2 * P] * len(keys))):
                 wu_codes[key] = (codes[:, x0:x1], plane[:, x0:x1])
 
         def round_u(raw, shares):
@@ -201,10 +202,14 @@ def tile_moe_prv_lin_bias_kernel(
             )
             return woven
 
+        def slot_codes(a, s0, s1):
+            start = max(first for b, first in s_codes if b == a and first <= s0)
+            return s_codes[a, start][:, s0 - start:s1 - start]
+
         def quantize_slots(a, s0, woven, widths):
             for x0, x1 in spans(widths):
                 nc.vector.quantize_mx(
-                    out=s_codes[:, a, s0 + x0:s0 + x1].bitcast(FP8X4),
+                    out=slot_codes(a, s0 + x0, s0 + x1).bitcast(FP8X4),
                     scales=s_plane[:, a, s0 + x0:s0 + x1],
                     in_=woven[:, 2 * x0:2 * x1].bitcast(BF16),
                 )
@@ -214,7 +219,7 @@ def tile_moe_prv_lin_bias_kernel(
                 out=bank[:],
                 lhsT=w_codes[:, expert_index * PASSES + a, :].bitcast(FP4X4),
                 lhsT_scale=w_plane[:, expert_index * PASSES + a, :],
-                rhs=s_codes[:, a, s0:s1].bitcast(FP8X4),
+                rhs=slot_codes(a, s0, s1).bitcast(FP8X4),
                 rhs_scale=s_plane[:, a, s0:s1],
                 start=(a == 0),
                 stop=(a == PASSES - 1),
@@ -272,10 +277,10 @@ def tile_moe_prv_lin_bias_kernel(
         def pairs_at(start, slots):
             return arena[:, start:start + 2 * slots].rearrange("p (h s) -> p h s", h=2)
 
-        first_pairs = [pairs_at(0, 640), pairs_at(3072, 768), pairs_at(0, 640)]
-        first_woven = arena[:, 1536:3072]
-        second_pairs = [pairs_at(4096, CHUNK), pairs_at(3072, CHUNK), pairs_at(0, CHUNK), pairs_at(4096, CHUNK)]
-        second_woven = keep.tile([P, 2 * CHUNK], U32, name="second_woven", align_bytes=64)[:]
+        first_pairs = [pairs_at(0, 768), pairs_at(3584, 768), pairs_at(0, 512)]
+        first_woven = arena[:, 2048:3584]
+        second_pairs = [pairs_at(4608, CHUNK), pairs_at(3584, CHUNK), pairs_at(0, CHUNK), pairs_at(4608, CHUNK)]
+        second_woven = [keep.tile([P, 2 * CHUNK], U32, name=f"second_woven{c}", align_bytes=64)[:] for c in range(2)]
 
         def gather_first(c):
             for h in range(2):
@@ -288,56 +293,65 @@ def tile_moe_prv_lin_bias_kernel(
         def gather_second(c):
             gather(second_pairs[c][:, 0, :], 1, 0, *SECOND_CHUNKS[c])
 
-        gather_first(0)
-        late = [
-            round_two([(1, 0, h, on_scalar), (1, 1, h, copy)], arena[:, x0:x0 + 1024].bitcast(BF16))
-            for h, x0, copy in ((1, 2304, on_vector), (0, 4096, on_scalar))
-        ]
-        quantize_wu(*late[0])
-        for t0, t1 in TOKEN_GROUPS:
+        earliest = arena[:, 1152:1664].bitcast(BF16)
+        round_wu(1, 0, 1, on_gpsimd, earliest, "p e m j")
+        latest = arena[:, 3456:4480].bitcast(BF16)
+        round_wu(1, 0, 0, on_scalar, latest[:, :2 * PASS])
+        middle = arena[:, 4864:5376].bitcast(BF16)
+        round_wu(1, 1, 1, on_scalar, middle)
+        round_wu(1, 1, 0, on_scalar, latest[:, 2 * PASS:])
+        gather(first_pairs[0][:, 0, :], 0, 0, 0, 768)
+        gather(first_pairs[0][:, 1, :384], 0, 1, 0, 384)
+        quantize_wu([(1, 0, 1)], earliest)
+        banks = [open_bank(1, 1, t0, t1) for t0, t1 in TOKEN_GROUPS[:2]]
+        gather(first_pairs[0][:, 1, 384:], 0, 1, 384, 768)
+        quantize_wu([(1, 1, 1)], middle)
+        for bank, (t0, t1) in zip(banks, TOKEN_GROUPS):
+            close_bank(bank, 1, 1, t0, t1)
+        for t0, t1 in TOKEN_GROUPS[2:]:
             project(1, 1, t0, t1)
-        gather(first_pairs[1][:, 0, :], 0, 0, *FIRST_CHUNKS[1])
-        weave_first(0)
-        quantize_wu(*late[1])
+        gather(first_pairs[1][:, 1, 512:], 0, 1, 1280, 1536)
+        quantize_wu([(1, 0, 0), (1, 1, 0)], latest)
         for t0, t1 in TOKEN_GROUPS:
             project(1, 0, t0, t1)
-        gather(first_pairs[1][:, 1, :], 0, 1, *FIRST_CHUNKS[1])
-        quantize_slots(0, 0, first_woven, [512, 128])
+        gather(first_pairs[1][:, 0, :], 0, 0, 768, 1536)
+        gather(first_pairs[1][:, 1, :512], 0, 1, 768, 1280)
+        weave_first(0)
+        quantize_slots(0, 0, first_woven, [512, 256])
         gather_first(2)
         weave_first(1)
         gather_rows(second_pairs[0][:, 1, :], *SECOND_CHUNKS[0])
-        quantize_slots(0, 640, first_woven, [512, 256])
-        gather_second(0)
-        gather_second(1)
-        gather_rows(second_pairs[1][:, 1, :], *SECOND_CHUNKS[1])
+        quantize_slots(0, 768, first_woven, [512, 256])
         weave_first(2)
-        gather_second(2)
-        gather_rows(second_pairs[2][:, 1, :], *SECOND_CHUNKS[2])
-        interleave(on_gpsimd, U32, second_woven, second_pairs[0])
-        quantize_slots(0, 1408, first_woven, [512, 128])
-        quantize_slots(1, 0, second_woven, [512])
+        for c in range(3):
+            gather_second(c)
+        for c in (1, 2):
+            gather_rows(second_pairs[c][:, 1, :], *SECOND_CHUNKS[c])
+        interleave(on_gpsimd, U32, second_woven[0], second_pairs[0])
         gather_second(3)
-        expert(0, True)
-        expert(1, True)
-        interleave(on_gpsimd, U32, second_woven, second_pairs[1])
-        for x0, x1 in spans([C, C]):
-            gather_rows(second_pairs[3][:, 1, x0:x1], 1536 + x0, 1536 + x1)
-        quantize_slots(1, 512, second_woven, [512])
+        interleave(on_gpsimd, U32, second_woven[1], second_pairs[1])
+        s_codes[0, 1536] = keep.tile([P, CHUNK], U32, name="x_pairs10", align_bytes=64)
+        quantize_slots(0, 1536, first_woven, [512])
+        quantize_slots(1, 0, second_woven[0], [512])
+        gather_rows(second_pairs[3][:, 1, :C], 1536, 1536 + C)
+        expert(0)
+        expert(1)
+        gather_rows(second_pairs[3][:, 1, C:], 1536 + C, S)
+        quantize_slots(1, 512, second_woven[1], [512])
         expert(2)
         expert(3)
-        last_woven = keep.tile([P, 4 * CHUNK], U32, name="x_pairs10", align_bytes=64)
-        interleave(on_vector, F32, last_woven[:, :1024], second_pairs[2])
+        interleave(on_vector, F32, second_woven[0], second_pairs[2])
         opened = [psum.tile([P, P], F32, name="bank") for c0 in range(0, C, P)]
         for bank, (s0, s1) in zip(opened, spans([S - C, P, P])[1:]):
             expert_pass(bank, E - 1, s0, s1, 0)
-        interleave(on_vector, F32, last_woven[:, 1024:1536], second_pairs[3][:, :, :C])
-        quantize_slots(1, 1024, last_woven, [512])
+        interleave(on_vector, F32, second_woven[1][:, :CHUNK], second_pairs[3][:, :, :C])
+        quantize_slots(1, 1024, second_woven[0], [512])
         expert(4)
-        expert(5)
-        interleave(on_vector, F32, last_woven[:, 1536:], second_pairs[3][:, :, C:])
-        quantize_slots(1, 1536, last_woven[:, 1024:], [256])
-        expert(6)
-        quantize_slots(1, 1792, last_woven[:, 1536:], [256])
+        interleave(on_vector, F32, second_woven[1][:, CHUNK:], second_pairs[3][:, :, C:])
+        quantize_slots(1, 1536, second_woven[1], [256])
+        quantize_slots(1, 1792, second_woven[1][:, CHUNK:], [256])
+        expert(5, True)
+        expert(6, True)
         for bank, (s0, s1) in zip(opened, spans([S - C, P, P])[1:]):
             expert_pass(bank, E - 1, s0, s1, 1)
             add_bias(bank, E - 1, s0, s1)

@@ -294,7 +294,7 @@ def tile_moe_prv_lin_bias_kernel(
             gather(second_pairs[c][:, 0, :], 1, 0, *SECOND_CHUNKS[c])
 
         earliest = arena[:, 1152:1664].bitcast(BF16)
-        round_wu(1, 0, 1, on_gpsimd, earliest, "p e m j")
+        round_wu(1, 0, 1, on_gpsimd, earliest, "p m e j")
         latest = arena[:, 3456:4480].bitcast(BF16)
         round_wu(1, 0, 0, on_scalar, latest[:, :2 * PASS])
         middle = arena[:, 4864:5376].bitcast(BF16)

@@ -43,6 +43,7 @@ LATE_LOADS = spans([512, 256, 128, 128])
 FIRST_BANKS = (spans([256, 256, 256, 128, 128]), TOKEN_GROUPS)
 FIRST_CHUNKS = spans([768, 768, 512])
 CHUNK = 512
+WARM_UPS = 4
 SECOND_CHUNKS = spans([CHUNK] * (S // CHUNK))
 OUT_CHUNKS = spans([320, 256, 256, 128, 64])
 
@@ -68,7 +69,7 @@ def tile_moe_prv_lin_bias_kernel(
             for a in range(PASSES)
             for f in range(PASSES)
         }
-        arena = keep.tile([P, 5632], U32, name="arena", align_bytes=64)
+        arena = keep.tile([P, 6144], U32, name="arena", align_bytes=64)
         u_early = keep.tile([P, PACK, T], F32, name="u_early")
         u_late = [keep.tile([P, PACK, t1 - t0], F32, name=f"u_late{i}") for i, (t0, t1) in enumerate(LATE_LOADS)]
         wu_codes = {}
@@ -270,7 +271,19 @@ def tile_moe_prv_lin_bias_kernel(
         close_first(1, 1, on_vector)
         close_first(0, 4, on_vector)
         close_first(1, 2)
-        project(0, 1, *TOKEN_GROUPS[-1])
+        last_bank = open_bank(0, 1, *TOKEN_GROUPS[-1])
+        close_bank(last_bank, 0, 1, *TOKEN_GROUPS[-1])
+        codes, plane = wu_codes[0, 1, 1]
+        for n in range(WARM_UPS):
+            nc.tensor.matmul_mx(
+                out=last_bank[:].rearrange("p e t -> p (e t)"),
+                lhsT=codes[:, :P].bitcast(FP8X4),
+                lhsT_scale=plane[:, :P],
+                rhs=u_codes[:, 1, :PASS].bitcast(FP8X4),
+                rhs_scale=u_plane[:, 1, :PASS],
+                start=True,
+                stop=True,
+            )
 
         on_gpsimd = nc.gpsimd.tensor_copy
 
@@ -279,7 +292,12 @@ def tile_moe_prv_lin_bias_kernel(
 
         first_pairs = [pairs_at(0, 768), pairs_at(3584, 768), pairs_at(0, 512)]
         first_woven = arena[:, 2048:3584]
-        second_pairs = [pairs_at(4608, CHUNK), pairs_at(3584, CHUNK), pairs_at(0, CHUNK), pairs_at(4608, CHUNK)]
+        second_pairs = [
+            pairs_at(4608, CHUNK),
+            pairs_at(3072, 1536)[:, :, 1024:],
+            pairs_at(512, CHUNK),
+            pairs_at(0, 1536)[:, :, :CHUNK],
+        ]
         second_woven = [keep.tile([P, 2 * CHUNK], U32, name=f"second_woven{c}", align_bytes=64)[:] for c in range(2)]
 
         def gather_first(c):
@@ -305,17 +323,18 @@ def tile_moe_prv_lin_bias_kernel(
         quantize_wu([(1, 0, 1)], earliest)
         banks = [open_bank(1, 1, t0, t1) for t0, t1 in TOKEN_GROUPS[:2]]
         gather(first_pairs[0][:, 1, 384:], 0, 1, 384, 768)
+        gather(first_pairs[1][:, 1, 256:384], 0, 1, 1024, 1152)
         quantize_wu([(1, 1, 1)], middle)
         for bank, (t0, t1) in zip(banks, TOKEN_GROUPS):
             close_bank(bank, 1, 1, t0, t1)
         for t0, t1 in TOKEN_GROUPS[2:]:
             project(1, 1, t0, t1)
-        gather(first_pairs[1][:, 1, 512:], 0, 1, 1280, 1536)
+        gather(first_pairs[1][:, 1, 384:], 0, 1, 1152, 1536)
         quantize_wu([(1, 0, 0), (1, 1, 0)], latest)
         for t0, t1 in TOKEN_GROUPS:
             project(1, 0, t0, t1)
         gather(first_pairs[1][:, 0, :], 0, 0, 768, 1536)
-        gather(first_pairs[1][:, 1, :512], 0, 1, 768, 1280)
+        gather(first_pairs[1][:, 1, :256], 0, 1, 768, 1024)
         weave_first(0)
         quantize_slots(0, 0, first_woven, [512, 256])
         gather_first(2)
@@ -323,20 +342,21 @@ def tile_moe_prv_lin_bias_kernel(
         gather_rows(second_pairs[0][:, 1, :], *SECOND_CHUNKS[0])
         quantize_slots(0, 768, first_woven, [512, 256])
         weave_first(2)
-        for c in range(3):
+        for c in range(4):
             gather_second(c)
         for c in (1, 2):
             gather_rows(second_pairs[c][:, 1, :], *SECOND_CHUNKS[c])
-        interleave(on_gpsimd, U32, second_woven[0], second_pairs[0])
-        gather_second(3)
-        interleave(on_gpsimd, U32, second_woven[1], second_pairs[1])
+        for c in range(2):
+            interleave(on_gpsimd, U32, second_woven[c], second_pairs[c])
         s_codes[0, 1536] = keep.tile([P, CHUNK], U32, name="x_pairs10", align_bytes=64)
         quantize_slots(0, 1536, first_woven, [512])
         quantize_slots(1, 0, second_woven[0], [512])
         gather_rows(second_pairs[3][:, 1, :C], 1536, 1536 + C)
+        interleave(on_scalar, F32, first_woven[:, :CHUNK], second_pairs[3][:, :, :C])
+        gather_rows(second_pairs[3][:, 1, C:], 1536 + C, S)
+        interleave(on_scalar, F32, first_woven[:, CHUNK:2 * CHUNK], second_pairs[3][:, :, C:])
         expert(0)
         expert(1)
-        gather_rows(second_pairs[3][:, 1, C:], 1536 + C, S)
         quantize_slots(1, 512, second_woven[1], [512])
         expert(2)
         expert(3)
@@ -344,12 +364,10 @@ def tile_moe_prv_lin_bias_kernel(
         opened = [psum.tile([P, P], F32, name="bank") for c0 in range(0, C, P)]
         for bank, (s0, s1) in zip(opened, spans([S - C, P, P])[1:]):
             expert_pass(bank, E - 1, s0, s1, 0)
-        interleave(on_vector, F32, second_woven[1][:, :CHUNK], second_pairs[3][:, :, :C])
         quantize_slots(1, 1024, second_woven[0], [512])
         expert(4)
-        interleave(on_vector, F32, second_woven[1][:, CHUNK:], second_pairs[3][:, :, C:])
-        quantize_slots(1, 1536, second_woven[1], [256])
-        quantize_slots(1, 1792, second_woven[1][:, CHUNK:], [256])
+        quantize_slots(1, 1536, first_woven, [256])
+        quantize_slots(1, 1792, first_woven[:, CHUNK:], [256])
         expert(5, True)
         expert(6, True)
         for bank, (s0, s1) in zip(opened, spans([S - C, P, P])[1:]):

@@ -117,11 +117,11 @@ def tile_moe_prv_lin_bias_kernel(
         on_vector = nc.vector.tensor_copy
         on_scalar = nc.scalar.copy
 
-        def round_wu(a, f, h, copy, grouped, order="p m j e"):
+        def round_wu(a, f, h, copy, grouped, order="p m j e", ms=slice(0, P)):
             columns = wu_raw[a, f].rearrange("p j (m h e) -> p j m h e", h=2, e=2)[:, :, :, h, :]
             copy(
-                out=grouped.rearrange("p (e m j) -> " + order, e=2, j=PACK),
-                in_=columns.rearrange("p j m e -> " + order),
+                out=grouped.rearrange("p (e m j) -> " + order, e=2, j=PACK)[:, ms],
+                in_=columns.rearrange("p j m e -> " + order)[:, ms],
             )
 
         def round_two(parts, grouped):
@@ -311,30 +311,31 @@ def tile_moe_prv_lin_bias_kernel(
         def gather_second(c):
             gather(second_pairs[c][:, 0, :], 1, 0, *SECOND_CHUNKS[c])
 
-        earliest = arena[:, 1152:1664].bitcast(BF16)
+        earliest = arena[:, 896:1408].bitcast(BF16)
         round_wu(1, 0, 1, on_gpsimd, earliest, "p m e j")
         latest = arena[:, 3456:4480].bitcast(BF16)
         round_wu(1, 0, 0, on_scalar, latest[:, :2 * PASS])
-        middle = arena[:, 4864:5376].bitcast(BF16)
-        round_wu(1, 1, 1, on_scalar, middle)
+        middle = arena[:, 1312:1824].bitcast(BF16)
+        round_wu(1, 1, 1, on_scalar, middle, ms=slice(48, P))
         round_wu(1, 1, 0, on_scalar, latest[:, 2 * PASS:])
         gather(first_pairs[0][:, 0, :], 0, 0, 0, 768)
-        gather(first_pairs[0][:, 1, :384], 0, 1, 0, 384)
+        gather(first_pairs[1][:, 1, 384:], 0, 1, 1152, 1536)
+        gather(first_pairs[0][:, 1, :128], 0, 1, 0, 128)
         quantize_wu([(1, 0, 1)], earliest)
+        round_wu(1, 1, 1, on_gpsimd, middle, "p m e j", slice(0, 48))
         banks = [open_bank(1, 1, t0, t1) for t0, t1 in TOKEN_GROUPS[:2]]
-        gather(first_pairs[0][:, 1, 384:], 0, 1, 384, 768)
-        gather(first_pairs[1][:, 1, 256:384], 0, 1, 1024, 1152)
+        gather(first_pairs[0][:, 1, 128:512], 0, 1, 128, 512)
         quantize_wu([(1, 1, 1)], middle)
         for bank, (t0, t1) in zip(banks, TOKEN_GROUPS):
             close_bank(bank, 1, 1, t0, t1)
         for t0, t1 in TOKEN_GROUPS[2:]:
             project(1, 1, t0, t1)
-        gather(first_pairs[1][:, 1, 384:], 0, 1, 1152, 1536)
+        gather(first_pairs[0][:, 1, 512:], 0, 1, 512, 768)
         quantize_wu([(1, 0, 0), (1, 1, 0)], latest)
         for t0, t1 in TOKEN_GROUPS:
             project(1, 0, t0, t1)
         gather(first_pairs[1][:, 0, :], 0, 0, 768, 1536)
-        gather(first_pairs[1][:, 1, :256], 0, 1, 768, 1024)
+        gather(first_pairs[1][:, 1, :384], 0, 1, 768, 1152)
         weave_first(0)
         quantize_slots(0, 0, first_woven, [512, 256])
         gather_first(2)
@@ -365,9 +366,9 @@ def tile_moe_prv_lin_bias_kernel(
         for bank, (s0, s1) in zip(opened, spans([S - C, P, P])[1:]):
             expert_pass(bank, E - 1, s0, s1, 0)
         quantize_slots(1, 1024, second_woven[0], [512])
-        expert(4)
         quantize_slots(1, 1536, first_woven, [256])
         quantize_slots(1, 1792, first_woven[:, CHUNK:], [256])
+        expert(4, True)
         expert(5, True)
         expert(6, True)
         for bank, (s0, s1) in zip(opened, spans([S - C, P, P])[1:]):

@@ -45,7 +45,7 @@ FIRST_CHUNKS = spans([768, 768, 512])
 CHUNK = 512
 WARM_UPS = 4
 SECOND_CHUNKS = spans([CHUNK] * (S // CHUNK))
-OUT_CHUNKS = spans([320, 256, 256, 128, 64])
+OUT_CHUNKS = spans([352, 256, 224, 128, 64])
 
 
 def tile_moe_prv_lin_bias_kernel(
@@ -66,10 +66,11 @@ def tile_moe_prv_lin_bias_kernel(
         w_plane = keep.tile([P, E * PASSES, N], U8, name="w_plane", align_bytes=64)
         wu_raw = {
             (a, f): keep.tile([P, PACK, PASS], F32, name=f"wu_raw{a}{f}", align_bytes=64)[:]
-            for a in range(PASSES)
-            for f in range(PASSES)
+            for a, f in ((0, 0), (0, 1))
         }
-        arena = keep.tile([P, 6144], U32, name="arena", align_bytes=64)
+        arena = keep.tile([P, 8320], U32, name="arena", align_bytes=64)
+        for f, x0 in enumerate((1152, 3200)):
+            wu_raw[1, f] = arena[:, x0:x0 + PACK * PASS].bitcast(F32).rearrange("p (j c) -> p j c", j=PACK)
         u_early = keep.tile([P, PACK, T], F32, name="u_early")
         u_late = [keep.tile([P, PACK, t1 - t0], F32, name=f"u_late{i}") for i, (t0, t1) in enumerate(LATE_LOADS)]
         wu_codes = {}
@@ -290,11 +291,11 @@ def tile_moe_prv_lin_bias_kernel(
         def pairs_at(start, slots):
             return arena[:, start:start + 2 * slots].rearrange("p (h s) -> p h s", h=2)
 
-        first_pairs = [pairs_at(0, 768), pairs_at(3584, 768), pairs_at(0, 512)]
-        first_woven = arena[:, 2048:3584]
+        first_pairs = [pairs_at(0, 768), pairs_at(4224, 768), pairs_at(0, 512)]
+        first_woven = arena[:, 6784:]
         second_pairs = [
-            pairs_at(4608, CHUNK),
-            pairs_at(3072, 1536)[:, :, 1024:],
+            pairs_at(5248, CHUNK),
+            pairs_at(3712, 1536)[:, :, 1024:],
             pairs_at(512, CHUNK),
             pairs_at(0, 1536)[:, :, :CHUNK],
         ]
@@ -311,31 +312,30 @@ def tile_moe_prv_lin_bias_kernel(
         def gather_second(c):
             gather(second_pairs[c][:, 0, :], 1, 0, *SECOND_CHUNKS[c])
 
-        earliest = arena[:, 896:1408].bitcast(BF16)
+        earliest = rounded_tile("rounded0")[:, :2 * PASS]
         round_wu(1, 0, 1, on_gpsimd, earliest, "p m e j")
-        latest = arena[:, 3456:4480].bitcast(BF16)
+        latest = arena[:, 6784:7808].bitcast(BF16)
         round_wu(1, 0, 0, on_scalar, latest[:, :2 * PASS])
-        middle = arena[:, 1312:1824].bitcast(BF16)
-        round_wu(1, 1, 1, on_scalar, middle, ms=slice(48, P))
+        middle = arena[:, 5504:6016].bitcast(BF16)
+        round_wu(1, 1, 1, on_scalar, middle)
         round_wu(1, 1, 0, on_scalar, latest[:, 2 * PASS:])
         gather(first_pairs[0][:, 0, :], 0, 0, 0, 768)
-        gather(first_pairs[1][:, 1, 384:], 0, 1, 1152, 1536)
-        gather(first_pairs[0][:, 1, :128], 0, 1, 0, 128)
+        gather(first_pairs[0][:, 1, :384], 0, 1, 0, 384)
+        gather(first_pairs[1][:, 1, 256:384], 0, 1, 1024, 1152)
         quantize_wu([(1, 0, 1)], earliest)
-        round_wu(1, 1, 1, on_gpsimd, middle, "p m e j", slice(0, 48))
         banks = [open_bank(1, 1, t0, t1) for t0, t1 in TOKEN_GROUPS[:2]]
-        gather(first_pairs[0][:, 1, 128:512], 0, 1, 128, 512)
+        gather(first_pairs[0][:, 1, 384:], 0, 1, 384, 768)
         quantize_wu([(1, 1, 1)], middle)
         for bank, (t0, t1) in zip(banks, TOKEN_GROUPS):
             close_bank(bank, 1, 1, t0, t1)
         for t0, t1 in TOKEN_GROUPS[2:]:
             project(1, 1, t0, t1)
-        gather(first_pairs[0][:, 1, 512:], 0, 1, 512, 768)
+        gather(first_pairs[1][:, 1, 384:], 0, 1, 1152, 1536)
         quantize_wu([(1, 0, 0), (1, 1, 0)], latest)
         for t0, t1 in TOKEN_GROUPS:
             project(1, 0, t0, t1)
         gather(first_pairs[1][:, 0, :], 0, 0, 768, 1536)
-        gather(first_pairs[1][:, 1, :384], 0, 1, 768, 1152)
+        gather(first_pairs[1][:, 1, :256], 0, 1, 768, 1024)
         weave_first(0)
         quantize_slots(0, 0, first_woven, [512, 256])
         gather_first(2)
@@ -349,26 +349,26 @@ def tile_moe_prv_lin_bias_kernel(
             gather_rows(second_pairs[c][:, 1, :], *SECOND_CHUNKS[c])
         for c in range(2):
             interleave(on_gpsimd, U32, second_woven[c], second_pairs[c])
-        s_codes[0, 1536] = keep.tile([P, CHUNK], U32, name="x_pairs10", align_bytes=64)
-        quantize_slots(0, 1536, first_woven, [512])
         quantize_slots(1, 0, second_woven[0], [512])
+        third_woven = interleave(on_vector, F32, arena[:, 5248:6272], second_pairs[2])
+        s_codes[0, 1536] = keep.tile([P, CHUNK], U32, name="second_woven0", align_bytes=64)
+        quantize_slots(0, 1536, first_woven, [512])
         gather_rows(second_pairs[3][:, 1, :C], 1536, 1536 + C)
-        interleave(on_scalar, F32, first_woven[:, :CHUNK], second_pairs[3][:, :, :C])
+        interleave(on_scalar, F32, second_pairs[1][:, 0, :], second_pairs[3][:, :, :C])
         gather_rows(second_pairs[3][:, 1, C:], 1536 + C, S)
-        interleave(on_scalar, F32, first_woven[:, CHUNK:2 * CHUNK], second_pairs[3][:, :, C:])
+        interleave(on_scalar, F32, second_pairs[1][:, 1, :], second_pairs[3][:, :, C:])
         expert(0)
         expert(1)
         quantize_slots(1, 512, second_woven[1], [512])
         expert(2)
         expert(3)
-        interleave(on_vector, F32, second_woven[0], second_pairs[2])
         opened = [psum.tile([P, P], F32, name="bank") for c0 in range(0, C, P)]
         for bank, (s0, s1) in zip(opened, spans([S - C, P, P])[1:]):
             expert_pass(bank, E - 1, s0, s1, 0)
-        quantize_slots(1, 1024, second_woven[0], [512])
-        quantize_slots(1, 1536, first_woven, [256])
-        quantize_slots(1, 1792, first_woven[:, CHUNK:], [256])
-        expert(4, True)
+        quantize_slots(1, 1024, third_woven, [512])
+        expert(4)
+        quantize_slots(1, 1536, second_pairs[1][:, 0, :], [256])
+        quantize_slots(1, 1792, second_pairs[1][:, 1, :], [256])
         expert(5, True)
         expert(6, True)
         for bank, (s0, s1) in zip(opened, spans([S - C, P, P])[1:]):
@@ -395,6 +395,8 @@ def tile_moe_prv_lin_bias_kernel(
             fetched = keep.tile([P, 2, t1 - t0], F32, name=f"fetched{i}")
             for choice, pos_sb in enumerate((pos1_sb, pos2_sb)):
                 nc.scalar.activation(out=fetched[:, choice, :], in_=positions(pos_sb, t0, t1), func=COPY)
+            last = i == len(OUT_CHUNKS) - 1
+            if last:
+                finish(*OUT_CHUNKS[i - 1])
             nc.vector.tensor_tensor(out=weighed[:, :, t0:t1], in0=fetched[:], in1=gates[:, :, t0:t1], op=MULT)
-            finish(*OUT_CHUNKS[i - 1])
-        finish(*OUT_CHUNKS[-1])
+            finish(*OUT_CHUNKS[i if last else i - 1])

@@ -356,7 +356,6 @@ def tile_moe_prv_lin_bias_kernel(
         gather_rows(second_pairs[3][:, 1, :C], 1536, 1536 + C)
         interleave(on_scalar, F32, second_pairs[1][:, 0, :], second_pairs[3][:, :, :C])
         gather_rows(second_pairs[3][:, 1, C:], 1536 + C, S)
-        interleave(on_scalar, F32, second_pairs[1][:, 1, :], second_pairs[3][:, :, C:])
         expert(0)
         expert(1)
         quantize_slots(1, 512, second_woven[1], [512])
@@ -367,6 +366,7 @@ def tile_moe_prv_lin_bias_kernel(
             expert_pass(bank, E - 1, s0, s1, 0)
         quantize_slots(1, 1024, third_woven, [512])
         expert(4)
+        interleave(on_vector, F32, second_pairs[1][:, 1, :], second_pairs[3][:, :, C:])
         quantize_slots(1, 1536, second_pairs[1][:, 0, :], [256])
         quantize_slots(1, 1792, second_pairs[1][:, 1, :], [256])
         expert(5, True)

@@ -45,7 +45,7 @@ FIRST_CHUNKS = spans([768, 768, 512])
 CHUNK = 512
 WARM_UPS = 4
 SECOND_CHUNKS = spans([CHUNK] * (S // CHUNK))
-OUT_CHUNKS = spans([352, 256, 224, 128, 64])
+OUT_CHUNKS = spans([384, 288, 192, 96, 64])
 
 
 def tile_moe_prv_lin_bias_kernel(
@@ -364,13 +364,17 @@ def tile_moe_prv_lin_bias_kernel(
         opened = [psum.tile([P, P], F32, name="bank") for c0 in range(0, C, P)]
         for bank, (s0, s1) in zip(opened, spans([S - C, P, P])[1:]):
             expert_pass(bank, E - 1, s0, s1, 0)
+        ahead = [psum.tile([P, C], F32, name="bank") for e in (5, 6)]
+        for e, bank in zip((5, 6), ahead):
+            expert_pass(bank, e, e * C, (e + 1) * C, 0)
         quantize_slots(1, 1024, third_woven, [512])
         expert(4)
         interleave(on_vector, F32, second_pairs[1][:, 1, :], second_pairs[3][:, :, C:])
         quantize_slots(1, 1536, second_pairs[1][:, 0, :], [256])
         quantize_slots(1, 1792, second_pairs[1][:, 1, :], [256])
-        expert(5, True)
-        expert(6, True)
+        for e, bank in zip((5, 6), ahead):
+            expert_pass(bank, e, e * C, (e + 1) * C, 1)
+            add_bias(bank, e, e * C, (e + 1) * C, True)
         for bank, (s0, s1) in zip(opened, spans([S - C, P, P])[1:]):
             expert_pass(bank, E - 1, s0, s1, 1)
             add_bias(bank, E - 1, s0, s1)
@@ -396,7 +400,7 @@ def tile_moe_prv_lin_bias_kernel(
             for choice, pos_sb in enumerate((pos1_sb, pos2_sb)):
                 nc.scalar.activation(out=fetched[:, choice, :], in_=positions(pos_sb, t0, t1), func=COPY)
             last = i == len(OUT_CHUNKS) - 1
-            if last:
-                finish(*OUT_CHUNKS[i - 1])
             nc.vector.tensor_tensor(out=weighed[:, :, t0:t1], in0=fetched[:], in1=gates[:, :, t0:t1], op=MULT)
-            finish(*OUT_CHUNKS[i if last else i - 1])
+            finish(*OUT_CHUNKS[i - 1])
+            if last:
+                finish(t0, t1)

from contextlib import ExitStack

import concourse.mybir as mybir

K, T, E, C, N, M = 1024, 1024, 8, 256, 128, 1024
S = E * C

FLOPS = 2 * M * K * T + 2 * K * N * S

F32 = mybir.dt.float32
BF16 = mybir.dt.bfloat16
I32 = mybir.dt.int32
U32 = mybir.dt.uint32
U16 = mybir.dt.uint16
U8 = mybir.dt.uint8
FP8X4 = mybir.dt.float8_e4m3fn_x4
FP4X4 = mybir.dt.float4_e2m1fn_x4
MULT = mybir.AluOpType.mult
ADD = mybir.AluOpType.add
COPY = mybir.ActivationFunctionType.Copy
IDENTITY = mybir.ActivationFunctionType.Identity

P = 128
PACK = 4
PASS = P * PACK
PASSES = 2
LIST_ROWS = 16
GROUP = 256
QUADRANTS = 4
RUN = 4


def spans(widths):
    out, start = [], 0
    for w in widths:
        out.append((start, start + w))
        start += w
    return out


TOKEN_GROUPS = spans([GROUP] * (T // GROUP))
LATE_LOADS = spans([512, 256, 128, 128])
FIRST_BANKS = (spans([256, 256, 256, 128, 128]), TOKEN_GROUPS)
FIRST_CHUNKS = spans([768, 768, 512])
CHUNK = 512
WARM_UPS = 4
SECOND_CHUNKS = spans([CHUNK] * (S // CHUNK))
OUT_CHUNKS = spans([384, 288, 192, 96, 64])


def tile_moe_prv_lin_bias_kernel(
    tc, uT, wu, w_words, w_scales, b, gate, offs, pos1, pos2, out
):
    nc = tc.nc
    with ExitStack() as ctx:
        keep = ctx.enter_context(tc.tile_pool(name="keep", bufs=1))
        stage = ctx.enter_context(tc.tile_pool(name="stage", bufs=4))
        psum = ctx.enter_context(tc.psum_pool(name="psum", bufs=8))

        offs_sb = keep.tile([P, S // LIST_ROWS], U16, name="offs_sb")
        pos1_sb = keep.tile([P, T // LIST_ROWS], U16, name="pos1_sb")
        pos2_sb = keep.tile([P, T // LIST_ROWS], U16, name="pos2_sb")
        bias = keep.tile([P, E], F32, name="bias")
        gates = keep.tile([P, 2, T], F32, name="gates")
        w_codes = keep.tile([P, E * PASSES, 2 * N], U8, name="w_codes", align_bytes=64)
        w_plane = keep.tile([P, E * PASSES, N], U8, name="w_plane", align_bytes=64)
        wu_raw = {
            (a, f): keep.tile([P, PACK, PASS], F32, name=f"wu_raw{a}{f}", align_bytes=64)[:]
            for a, f in ((0, 0), (0, 1))
        }
        arena = keep.tile([P, 8320], U32, name="arena", align_bytes=64)
        for f, x0 in enumerate((1152, 3200)):
            wu_raw[1, f] = arena[:, x0:x0 + PACK * PASS].bitcast(F32).rearrange("p (j c) -> p j c", j=PACK)
        u_early = keep.tile([P, PACK, T], F32, name="u_early")
        u_late = [keep.tile([P, PACK, t1 - t0], F32, name=f"u_late{i}") for i, (t0, t1) in enumerate(LATE_LOADS)]
        wu_codes = {}
        u_codes = keep.tile([P, PASSES, T], U32, name="u_codes", align_bytes=64)
        u_plane = keep.tile([P, PASSES, T], U8, name="u_plane", align_bytes=64)
        x_pairs = {(a, h): keep.tile([P, T], U32, name=f"x_pairs{a}{h}", align_bytes=64) for a, h in ((0, 0), (0, 1), (1, 0))}
        x_rows = keep.tile([P, 2, T], BF16, name="x_rows", align_bytes=64)
        s_codes = {(a, 0): keep.tile([P, S], U32, name=f"s_codes{a}", align_bytes=64) for a in range(PASSES)}
        s_plane = keep.tile([P, PASSES, S], U8, name="s_plane", align_bytes=64)
        y = keep.tile([P, S], F32, name="y")
        weighed = keep.tile([P, 2, T], F32, name="weighed")
        total = keep.tile([P, T], F32, name="total")

        nc.vector.memset(w_plane[:].rearrange("p g n -> p (g n)").bitcast(I32), 0)

        def load_wu(a, f):
            rows = wu[f * PASS:(f + 1) * PASS, a * PASS:(a + 1) * PASS]
            nc.sync.dma_start(out=wu_raw[a, f], in_=rows.rearrange("(p j) c -> p j c", j=PACK))

        def load_u(raw, f, t0, t1):
            rows = uT[f * PASS:(f + 1) * PASS, t0:t1]
            nc.sync.dma_start(out=raw[:], in_=rows.rearrange("(p j) t -> p j t", j=PACK))

        load_wu(0, 0)
        load_u(u_early, 0, 0, T)
        load_wu(0, 1)
        for raw, (t0, t1) in zip(u_late, LATE_LOADS):
            load_u(raw, 1, t0, t1)
        nc.sync.dma_start(offs_sb[:], offs)
        for f in range(PASSES):
            load_wu(1, f)
        nc.sync.dma_start(
            out=w_codes[:].bitcast(I32), in_=w_words.rearrange("e a p b -> p (e a) b").bitcast(I32)
        )
        scale_rows = w_scales.rearrange("e a q n -> q (e a) n").bitcast(I32)
        for quad in range(QUADRANTS):
            nc.sync.dma_start(
                out=w_plane[32 * quad:32 * quad + 4, :, :].bitcast(I32), in_=scale_rows[4 * quad:4 * quad + 4]
            )
        nc.sync.dma_start(out=bias[:], in_=b)
        nc.sync.dma_start(pos1_sb[:], pos1)
        nc.sync.dma_start(pos2_sb[:], pos2)
        nc.sync.dma_start(out=gates[:], in_=gate.rearrange("g p t -> p g t"))

        on_vector = nc.vector.tensor_copy
        on_scalar = nc.scalar.copy

        def round_wu(a, f, h, copy, grouped, order="p m j e", ms=slice(0, P)):
            columns = wu_raw[a, f].rearrange("p j (m h e) -> p j m h e", h=2, e=2)[:, :, :, h, :]
            copy(
                out=grouped.rearrange("p (e m j) -> " + order, e=2, j=PACK)[:, ms],
                in_=columns.rearrange("p j m e -> " + order)[:, ms],
            )

        def round_two(parts, grouped):
            for (a, f, h, copy), (x0, x1) in zip(parts, spans([2 * PASS] * 2)):
                round_wu(a, f, h, copy, grouped[:, x0:x1])
            return [part[:3] for part in parts], grouped

        def rounded_tile(name):
            return keep.tile([P, PACK * PASS], BF16, name=name, align_bytes=64)[:]

        def quantize_wu(keys, grouped):
            name = "%d%d%d" % keys[0]
            codes = keep.tile([P, 2 * P * len(keys)], U32, name="wu_codes" + name, align_bytes=64)
            plane = keep.tile([P, 2 * P * len(keys)], U8, name="wu_plane" + name, align_bytes=64)
            nc.vector.quantize_mx(out=codes[:].bitcast(FP8X4), scales=plane[:], in_=grouped)
            for key, (x0, x1) in zip(keys, spans([2 * P] * len(keys))):
                wu_codes[key] = (codes[:, x0:x1], plane[:, x0:x1])

        def round_u(raw, shares):
            grouped = stage.tile([P, PACK * raw.shape[2]], BF16, name="narrow", align_bytes=64)
            for copy, (t0, t1) in zip([c for c, w in shares], spans([w for c, w in shares])):
                copy(
                    out=grouped[:, PACK * t0:PACK * t1].rearrange("p (c i j) -> p c j i", i=RUN, j=PACK),
                    in_=raw[:, :, t0:t1].rearrange("p j (c i) -> p c j i", i=RUN),
                )
            return grouped

        def quantize_u(f, t0, t1, grouped):
            nc.vector.quantize_mx(out=u_codes[:, f, t0:t1].bitcast(FP8X4), scales=u_plane[:, f, t0:t1], in_=grouped[:])

        def project_pass(bank, a, h, e, f, t0, t1, start, stop):
            codes, plane = wu_codes[a, f, h]
            cols = slice(e * P, (e + 1) * P)
            nc.tensor.matmul_mx(
                out=bank[:, e, :],
                lhsT=codes[:, cols].bitcast(FP8X4),
                lhsT_scale=plane[:, cols],
                rhs=u_codes[:, f, t0:t1].bitcast(FP8X4),
                rhs_scale=u_plane[:, f, t0:t1],
                start=start,
                stop=stop,
            )

        def open_bank(a, h, t0, t1):
            bank = psum.tile([P, 2, t1 - t0], F32, name="bank")
            for e in range(2):
                project_pass(bank, a, h, e, 0, t0, t1, e == 0, False)
            return bank

        def close_bank(bank, a, h, t0, t1, copy=on_scalar):
            for e in range(2):
                project_pass(bank, a, h, e, 1, t0, t1, False, e == 1)
            if (a, h) in x_pairs:
                copy(
                    out=x_pairs[a, h][:, t0:t1].bitcast(BF16).rearrange("p (t e) -> p t e", e=2),
                    in_=bank[:].rearrange("p e t -> p t e"),
                )
            else:
                copy(out=x_rows[:, :, t0:t1], in_=bank[:])

        def project(a, h, t0, t1):
            close_bank(open_bank(a, h, t0, t1), a, h, t0, t1)

        def offsets(s0, s1):
            return offs_sb[:, s0 // LIST_ROWS:s1 // LIST_ROWS]

        def gather(dst, a, h, s0, s1):
            nc.vector.tensor_copy(out=dst, in_=x_pairs[a, h][:].indirect(offsets(s0, s1)))

        def gather_rows(dst, s0, s1):
            halves = dst.bitcast(BF16).rearrange("p (s e) -> p e s", e=2)
            for e in range(2):
                nc.scalar.activation(out=halves[:, e, :], in_=x_rows[:, e, :].indirect(offsets(s0, s1)), func=COPY)

        def interleave(copy, word, woven, pairs):
            copy(
                out=woven.bitcast(word).rearrange("p (s h) -> p s h", h=2),
                in_=pairs.bitcast(word).rearrange("p h s -> p s h"),
            )
            return woven

        def slot_codes(a, s0, s1):
            start = max(first for b, first in s_codes if b == a and first <= s0)
            return s_codes[a, start][:, s0 - start:s1 - start]

        def quantize_slots(a, s0, woven, widths):
            for x0, x1 in spans(widths):
                nc.vector.quantize_mx(
                    out=slot_codes(a, s0 + x0, s0 + x1).bitcast(FP8X4),
                    scales=s_plane[:, a, s0 + x0:s0 + x1],
                    in_=woven[:, 2 * x0:2 * x1].bitcast(BF16),
                )

        def expert_pass(bank, expert_index, s0, s1, a):
            nc.tensor.matmul_mx(
                out=bank[:],
                lhsT=w_codes[:, expert_index * PASSES + a, :].bitcast(FP4X4),
                lhsT_scale=w_plane[:, expert_index * PASSES + a, :],
                rhs=slot_codes(a, s0, s1).bitcast(FP8X4),
                rhs_scale=s_plane[:, a, s0:s1],
                start=(a == 0),
                stop=(a == PASSES - 1),
            )

        def add_bias(bank, expert_index, s0, s1, on_vector_engine=False):
            column = bias[:, expert_index:expert_index + 1]
            if on_vector_engine:
                nc.vector.tensor_scalar(out=y[:, s0:s1], in0=bank[:], scalar1=column, scalar2=None, op0=ADD)
            else:
                nc.scalar.activation(out=y[:, s0:s1], in_=bank[:], func=IDENTITY, bias=column)

        def expert(expert_index, on_vector_engine=False):
            s0, s1 = expert_index * C, (expert_index + 1) * C
            bank = psum.tile([P, C], F32, name="bank")
            for a in range(PASSES):
                expert_pass(bank, expert_index, s0, s1, a)
            add_bias(bank, expert_index, s0, s1, on_vector_engine)

        quantize_wu(*round_two([(0, 0, 0, on_scalar), (0, 0, 1, on_vector)], rounded_tile("rounded0")))
        early = [round_u(u_early[:, :, t0:t1], [(on_scalar, 192), (on_vector, 320)]) for t0, t1 in spans([T // 2] * 2)]
        for grouped, (t0, t1) in zip(early, spans([T // 2] * 2)):
            quantize_u(0, t0, t1, grouped)
        banks = {(h, t0): open_bank(0, h, t0, t1) for h in range(2) for t0, t1 in FIRST_BANKS[h][:5 - 2 * h]}
        quantize_wu(*round_two([(0, 1, 0, on_scalar), (0, 1, 1, on_vector)], rounded_tile("rounded1")))

        def close_first(h, i, copy=on_scalar):
            t0, t1 = FIRST_BANKS[h][i]
            close_bank(banks[h, t0], 0, h, t0, t1, copy)

        ranges = FIRST_BANKS[0]
        late = [
            round_u(u_late[0][:, :, :GROUP], [(on_vector, GROUP)]),
            round_u(u_late[0][:, :, GROUP:], [(on_scalar, GROUP)]),
        ]
        quantize_u(1, *ranges[0], late[0])
        close_first(0, 0)
        late.append(round_u(u_late[1][:], [(on_vector, GROUP)]))
        quantize_u(1, *ranges[1], late[1])
        close_first(0, 1)
        close_first(1, 0)
        quantize_u(1, *ranges[2], late[2])
        close_first(0, 2)
        late.extend(round_u(raw[:], [(on_vector, GROUP // 2)]) for raw in u_late[2:])
        quantize_u(1, *ranges[3], late[3])
        close_first(0, 3)
        quantize_u(1, *ranges[4], late[4])
        close_first(1, 1, on_vector)
        close_first(0, 4, on_vector)
        close_first(1, 2)
        last_bank = open_bank(0, 1, *TOKEN_GROUPS[-1])
        close_bank(last_bank, 0, 1, *TOKEN_GROUPS[-1])
        codes, plane = wu_codes[0, 1, 1]
        for n in range(WARM_UPS):
            nc.tensor.matmul_mx(
                out=last_bank[:].rearrange("p e t -> p (e t)"),
                lhsT=codes[:, :P].bitcast(FP8X4),
                lhsT_scale=plane[:, :P],
                rhs=u_codes[:, 1, :PASS].bitcast(FP8X4),
                rhs_scale=u_plane[:, 1, :PASS],
                start=True,
                stop=True,
            )

        on_gpsimd = nc.gpsimd.tensor_copy

        def pairs_at(start, slots):
            return arena[:, start:start + 2 * slots].rearrange("p (h s) -> p h s", h=2)

        first_pairs = [pairs_at(0, 768), pairs_at(4224, 768), pairs_at(0, 512)]
        first_woven = arena[:, 6784:]
        second_pairs = [
            pairs_at(5248, CHUNK),
            pairs_at(3712, 1536)[:, :, 1024:],
            pairs_at(512, CHUNK),
            pairs_at(0, 1536)[:, :, :CHUNK],
        ]
        second_woven = [keep.tile([P, 2 * CHUNK], U32, name=f"second_woven{c}", align_bytes=64)[:] for c in range(2)]

        def gather_first(c):
            for h in range(2):
                gather(first_pairs[c][:, h, :], 0, h, *FIRST_CHUNKS[c])

        def weave_first(c):
            s0, s1 = FIRST_CHUNKS[c]
            interleave(on_gpsimd, U32, first_woven[:, :2 * (s1 - s0)], first_pairs[c])

        def gather_second(c):
            gather(second_pairs[c][:, 0, :], 1, 0, *SECOND_CHUNKS[c])

        earliest = rounded_tile("rounded0")[:, :2 * PASS]
        round_wu(1, 0, 1, on_gpsimd, earliest, "p m e j")
        latest = arena[:, 6784:7808].bitcast(BF16)
        round_wu(1, 0, 0, on_scalar, latest[:, :2 * PASS])
        middle = arena[:, 5504:6016].bitcast(BF16)
        round_wu(1, 1, 1, on_scalar, middle)
        round_wu(1, 1, 0, on_scalar, latest[:, 2 * PASS:])
        gather(first_pairs[0][:, 0, :], 0, 0, 0, 768)
        gather(first_pairs[0][:, 1, :384], 0, 1, 0, 384)
        gather(first_pairs[1][:, 1, 256:384], 0, 1, 1024, 1152)
        quantize_wu([(1, 0, 1)], earliest)
        banks = [open_bank(1, 1, t0, t1) for t0, t1 in TOKEN_GROUPS[:2]]
        gather(first_pairs[0][:, 1, 384:], 0, 1, 384, 768)
        quantize_wu([(1, 1, 1)], middle)
        for bank, (t0, t1) in zip(banks, TOKEN_GROUPS):
            close_bank(bank, 1, 1, t0, t1)
        for t0, t1 in TOKEN_GROUPS[2:]:
            project(1, 1, t0, t1)
        gather(first_pairs[1][:, 1, 384:], 0, 1, 1152, 1536)
        quantize_wu([(1, 0, 0), (1, 1, 0)], latest)
        for t0, t1 in TOKEN_GROUPS:
            project(1, 0, t0, t1)
        gather(first_pairs[1][:, 0, :], 0, 0, 768, 1536)
        gather(first_pairs[1][:, 1, :256], 0, 1, 768, 1024)
        weave_first(0)
        quantize_slots(0, 0, first_woven, [512, 256])
        gather_first(2)
        weave_first(1)
        gather_rows(second_pairs[0][:, 1, :], *SECOND_CHUNKS[0])
        quantize_slots(0, 768, first_woven, [512, 256])
        weave_first(2)
        for c in range(4):
            gather_second(c)
        for c in (1, 2):
            gather_rows(second_pairs[c][:, 1, :], *SECOND_CHUNKS[c])
        for c in range(2):
            interleave(on_gpsimd, U32, second_woven[c], second_pairs[c])
        quantize_slots(1, 0, second_woven[0], [512])
        third_woven = interleave(on_vector, F32, arena[:, 5248:6272], second_pairs[2])
        s_codes[0, 1536] = keep.tile([P, CHUNK], U32, name="second_woven0", align_bytes=64)
        quantize_slots(0, 1536, first_woven, [512])
        gather_rows(second_pairs[3][:, 1, :C], 1536, 1536 + C)
        interleave(on_scalar, F32, second_pairs[1][:, 0, :], second_pairs[3][:, :, :C])
        gather_rows(second_pairs[3][:, 1, C:], 1536 + C, S)
        expert(0)
        expert(1)
        quantize_slots(1, 512, second_woven[1], [512])
        expert(2)
        expert(3)
        opened = [psum.tile([P, P], F32, name="bank") for c0 in range(0, C, P)]
        for bank, (s0, s1) in zip(opened, spans([S - C, P, P])[1:]):
            expert_pass(bank, E - 1, s0, s1, 0)
        ahead = [psum.tile([P, C], F32, name="bank") for e in (5, 6)]
        for e, bank in zip((5, 6), ahead):
            expert_pass(bank, e, e * C, (e + 1) * C, 0)
        quantize_slots(1, 1024, third_woven, [512])
        expert(4)
        interleave(on_vector, F32, second_pairs[1][:, 1, :], second_pairs[3][:, :, C:])
        quantize_slots(1, 1536, second_pairs[1][:, 0, :], [256])
        quantize_slots(1, 1792, second_pairs[1][:, 1, :], [256])
        for e, bank in zip((5, 6), ahead):
            expert_pass(bank, e, e * C, (e + 1) * C, 1)
            add_bias(bank, e, e * C, (e + 1) * C, True)
        for bank, (s0, s1) in zip(opened, spans([S - C, P, P])[1:]):
            expert_pass(bank, E - 1, s0, s1, 1)
            add_bias(bank, E - 1, s0, s1)

        def positions(pos_sb, t0, t1):
            return y[:].indirect(pos_sb[:, t0 // LIST_ROWS:t1 // LIST_ROWS])

        def finish(t0, t1):
            nc.vector.tensor_tensor(out=total[:, t0:t1], in0=weighed[:, 0, t0:t1], in1=weighed[:, 1, t0:t1], op=ADD)
            nc.sync.dma_start(out=out[:, t0:t1], in_=total[:, t0:t1])

        for i, (t0, t1) in enumerate(OUT_CHUNKS):
            if i == 0:
                for choice, pos_sb in enumerate((pos1_sb, pos2_sb)):
                    nc.vector.tensor_tensor(
                        out=weighed[:, choice, t0:t1],
                        in0=positions(pos_sb, t0, t1),
                        in1=gates[:, choice, t0:t1],
                        op=MULT,
                    )
                continue
            fetched = keep.tile([P, 2, t1 - t0], F32, name=f"fetched{i}")
            for choice, pos_sb in enumerate((pos1_sb, pos2_sb)):
                nc.scalar.activation(out=fetched[:, choice, :], in_=positions(pos_sb, t0, t1), func=COPY)
            last = i == len(OUT_CHUNKS) - 1
            nc.vector.tensor_tensor(out=weighed[:, :, t0:t1], in0=fetched[:], in1=gates[:, :, t0:t1], op=MULT)
            finish(*OUT_CHUNKS[i - 1])
            if last:
                finish(t0, t1)
